import numpy as np, ml_dtypes
CORES = [2,3,42,43,82,83,122,123]
N = 8
BF = ml_dtypes.bfloat16
C, S, M, B, LB, A, CL = 4, 4096, 8, 128, 7, 20, 255
def fold(p):
    p = np.asarray(p, np.int64)[..., None, None]; n = np.arange(M)[:, None]; b = np.arange(B)[None, :]
    return ((n * p + b * (p >> LB)) >> 8).reshape(p.shape[:-2] + (M * B,))
def bend(t, a):
    return t + ((a * (t >> 3) ** 2) >> 12)
def trials(rng, a, h):
    v = bend(np.arange(S, dtype=np.int64), a[..., None]); last = np.sum(np.maximum.accumulate(v, -1) < S, -1) - 1
    p = np.maximum(256 * (last + 1) * h // (64 * M), 256); room = last - fold(p)[..., -1]
    return p, rng.integers(0, room[..., None] + 1, (N, 8, N * C)), room
def given(x, p, a, de):
    return {"x": x.reshape(N, 16, C * S).astype(np.float32).astype(BF), "pa": np.stack([p, a], -1).astype(np.int32), "de": de.astype(np.int32)}
def setup_inputs(rng):
    a = rng.integers(-A, A + 1, (N, 8)); p, de, room = trials(rng, a, rng.integers(32, 58, (N, 8)))
    return given(rng.integers(0, 16, (N, 16, C, S)), p, a, de)
def setup_inputs_ends(rng):
    a = rng.permuted(np.tile(np.array([-A, -A, -1, 0, 0, 1, A, A]), (N, 1)), axis=1)
    h = rng.permuted(np.tile(np.array([0, 0, 20, 40, 40, 60, 64, 64]), (N, 1)), axis=1)
    p, de, room = trials(rng, a, h); far = rng.permuted(np.tile(np.arange(N * C) % 2, (N, 8, 1)), axis=2)
    return given(rng.integers(0, 16, (N, 16, C, S)), p, a, far * room[..., None])
def setup_inputs_brink(rng):
    a = rng.integers(-A, A + 1, (N, 8)); p, de, room = trials(rng, a, rng.integers(32, 58, (N, 8)))
    u = rng.integers(0, 8, (N, 16, C, S)); return given(8 + (u == 0) - 1 * (u == 1), p, a, de)
def setup_inputs_alike(rng):
    a = np.repeat(rng.integers(-A, A + 1, (N, 1)), 8, axis=1); p, de, room = trials(rng, a, np.repeat(rng.integers(16, 61, (N, 1)), 8, axis=1))
    q = rng.integers(0, N); de[q] = de[q, :1]; return given(rng.integers(0, 16, (N, 16, C, S)), p, a, de)
def setup_inputs_spread(rng):
    a = rng.integers(-A, A + 1, (N, 8)); p, de, room = trials(rng, a, rng.integers(1, 65, (N, 8)))
    v = rng.integers(0, 16, (N, 16, C, S)); m = rng.integers(0, 16, (N, 16, C, 1)); up = rng.permutation(np.arange(16) % 2).reshape(1, 16, 1, 1)
    v = np.where(up == 1, np.maximum(v, m), np.minimum(v, m)); k = rng.permutation(16)[:3]; v[:, k[:2]] = 15; v[:, k[2]] = 0
    return given(v, p, a, de)
def check_inputs(d):
    try:
        bad = []; x = np.asarray(d["x"]).astype(np.float32); pa = np.asarray(d["pa"]).astype(np.int64); de = np.asarray(d["de"]).astype(np.int64)
        if x.shape != (N, 16, C * S) or pa.shape != (N, 8, 2) or de.shape != (N, 8, N * C): return ["shapes"]
        if not (np.isfinite(x).all() and (x == np.floor(x)).all() and x.min() >= 0 and x.max() <= 15): bad.append("samples")
        if pa[..., 0].min() < 256: bad.append("periods")
        if np.abs(pa[..., 1]).max() > A: bad.append("accelerations")
        if de.min() < 0: bad.append("delays")
        t = fold(pa[..., 0])[:, :, None, :] + de[..., None]
        if t.min() < 0 or t.max() >= S: bad.append("times")
        s = bend(t, pa[..., 1][:, :, None, None])
        if s.min() < 0 or s.max() >= S: bad.append("places")
        return bad
    except Exception:
        return ["form"]
def reference(x, pa, de):
    v = x.astype(np.float32).astype(np.int64).reshape(N, 16, C, S); y = np.zeros((N, 8, 16, B), np.int64)
    for r in range(N):
        for g in range(8):
            fp = fold(pa[r, g, 0]); a = int(pa[r, g, 1]); tot = np.zeros((16, M * B), np.int64)
            for q in range(N):
                for c in range(C):
                    tot += v[q, :, c][:, bend(fp + int(de[r, g, C * q + c]), a)]
            y[r, g] = np.add.reduce(np.minimum(tot, CL).reshape(16, M, B), axis=1)
    return {"y": y.reshape(N, 128, B).astype(np.float32)}

@@ -1,0 +1,485 @@
+from concourse.bass import DstId, RemoteDMATransfer
+from concourse.mybir import AluOpType as Op, ActivationFunctionType as Act
+
+MAGIC = 12582912.0
+HALF = 2047.5 / 4096.0
+CH = 4096
+KAPPA = 1.6
+FIRST = 3
+OWN_CHUNKS = (((0,), (-9, -9, -8.998, -8.997)), ((1,), (-8.9, -8.9, -8.898, -8.897)), ((2, 3), (-8.8, 0.2, 1.2, 1.6)))
+FIRST_CHUNKS = (((0, 1), (1.3, 1.8, 2.6, 2.7)), ((2, 3), (1.31, 2.3, 3.6, 4.1)))
+LATER_CHUNKS = (-8.2, -6.8, -5.9, -4.7)
+BLOCKS = ((0, 1), (2, 3))
+GROUPS = ((0, 1), (2,), (3,))
+EVAC, EVAC3 = 2.7, 1.6
+CREDIT = 3000.0
+
+SCRATCH = {
+    "wo": ("sbuf", [128, CH], "bfloat16"), "ws": ("sbuf", [128, CH], "bfloat16"),
+    "raw": ("sbuf", [128, 4], "int32"), "pf": ("sbuf", [128, 4], "float32"), "ones": ("sbuf", [128, 4], "float32"),
+    "hq": ("sbuf", [128, 1], "int32"), "lr": ("sbuf", [128, 1], "int32"),
+    "a0": ("sbuf", [128, 1], "float32"), "a1": ("sbuf", [128, 1], "float32"),
+    "mi": ("sbuf", [128, 4], "int32"), "x17": ("sbuf", [128, 1], "int32"), "x48": ("sbuf", [128, 1], "int32"),
+    "x49": ("sbuf", [128, 1], "int32"), "m0": ("sbuf", [128, 1], "float32"), "m1": ("sbuf", [128, 1], "float32"),
+    "selr": ("sbuf", [128, 1], "float32"), "selq": ("sbuf", [128, 1], "float32"), "one1": ("sbuf", [128, 1], "float32"),
+    "sa": ("sbuf", [128, 1], "float32"), "sb": ("sbuf", [128, 1], "float32"), "sc": ("sbuf", [128, 1], "float32"),
+    "ic": ("sbuf", [128, 32], "int32"), "cm": ("sbuf", [128, 32], "float32"),
+    "itr": ("sbuf", [128, 32], "float32"), "itk": ("sbuf", [128, 32], "float32"), "itm": ("sbuf", [128, 32], "float32"),
+    "ie": ("sbuf", [128, 4], "int32"), "iee": ("sbuf", [128, 4], "int32"), "ie2": ("sbuf", [128, 4], "int32"),
+    "io1": ("sbuf", [128, 4], "int32"), "oa": ("sbuf", [128, 4], "float32"), "ob": ("sbuf", [128, 4], "float32"),
+    "ea": ("sbuf", [128, 4], "float32"), "eb": ("sbuf", [128, 4], "float32"), "e2": ("sbuf", [128, 4], "float16"),
+    "jf": ("sbuf", [128, 128], "int32"), "f": ("sbuf", [128, 128], "float32"),
+    "fc": ("sbuf", [128, 64], "float32"), "fn": ("sbuf", [128, 64], "float32"),
+    "rha": ("sbuf", [128, 512], "float16"), "rhb": ("sbuf", [128, 512], "float16"),
+    "l0": ("sbuf", [128, 128], "float16"), "lin": ("sbuf", [128, 512], "float16"),
+    "mg": ("sbuf", [128, 512], "bfloat16"), "zer": ("sbuf", [128, 256], "bfloat16"),
+    "isel": ("sbuf", [128, 32], "int32"), "sel1": ("sbuf", [128, 32], "bfloat16"), "sel2": ("sbuf", [128, 32], "bfloat16"),
+    "isel2": ("sbuf", [128, 16], "int32"), "selb": ("sbuf", [128, 16], "bfloat16"), "onesb": ("sbuf", [128, 128], "bfloat16"),
+    "gall": ("sbuf", [128, 32768], "bfloat16"),
+    "acc": ("sbuf", [128, 512], "float32"), "tot": ("sbuf", [128, 512], "int32"),
+    "ta": ("sbuf", [128, 512], "int32"), "tb": ("sbuf", [128, 512], "int32"),
+    "ca": ("sbuf", [128, 512], "bfloat16"), "cb": ("sbuf", [128, 512], "bfloat16"),
+    "ysb": ("sbuf", [128, 128], "float32"),
+}
+for _n in ("A0", "A1", "B0", "B1", "s0", "s1", "xb", "yp"):
+    SCRATCH[_n] = ("psum", [128, 512], "float32")
+for _d in range(4):
+    for _n, _t in (("w", "float32"), ("z", "float32"), ("v", "float32"), ("off", "uint16")):
+        SCRATCH["%s%d" % (_n, _d)] = ("sbuf", [128, 512], _t)
+    SCRATCH["as%d" % _d] = ("sbuf", [128, 4], "float32")
+    if _d:
+        SCRATCH["snd%d" % _d] = ("sbuf", [128, 512], "uint16")
+        SCRATCH["rcv%d" % _d] = ("sbuf", [128, 512], "uint16")
+SEMAPHORES = ["V", "S", "P", "G", "par", "xl", "xs", "xr", "ps", "out", "sent"] + ["pr%d" % k for k in range(4)] \
+    + ["ar%d%d" % (d, b) for d in range(1, 4) for b in range(len(BLOCKS))]
+
+
+def rank_program(g, core, T, topo):
+    me = T.rank_of(core)
+    if me is None:
+        return
+    cores = list(T.cores)
+    chips = []
+    for c in cores:
+        if topo.chip(c) not in chips:
+            chips.append(topo.chip(c))
+    on = [[c for c in cores if topo.chip(c) == ch] for ch in chips]
+    k = chips.index(topo.chip(core))
+    pos = on[k].index(core)
+    sib = [c for c in on[k] if c != core][0]
+    q0, q1 = me, T.rank_of(sib)
+    peer = [on[(k + d) % 4][pos] for d in range(4)]
+
+    V, S, P = g.vector, g.scalar, g.tensor
+    queue = {"V": V, "S": S, "P": P, "G": g, "Y": g.sync}
+    cnt = {"V": 0, "S": 0, "P": 0, "G": 0}
+    seen = {}
+
+    def em(E, ins):
+        ins.then_inc(T.sem[E], 1)
+        cnt[E] += 1
+        return (E, cnt[E])
+
+    def need(E, *toks):
+        best = {}
+        for tk in toks:
+            if tk is not None:
+                best[tk[0]] = max(best.get(tk[0], 0), tk[1])
+        for s in best:
+            if seen.get((E, s), 0) < best[s]:
+                queue[E].wait_ge(T.sem[s], best[s])
+                seen[(E, s)] = best[s]
+
+    def gcomp(fn, *a, **kw):
+        need("G", ("G", cnt["G"]))
+        return em("G", fn(*a, **kw))
+
+    def vs(needs, out, in0, s1, s2, op0, op1=None):
+        need("V", *needs)
+        if op1 is None:
+            return em("V", V.tensor_scalar(out, in0, s1, None, op0))
+        return em("V", V.tensor_scalar(out, in0, s1, s2, op0, op1))
+
+    def vt(needs, out, in0, in1, op):
+        need("V", *needs)
+        return em("V", V.tensor_tensor(out, in0, in1, op))
+
+    for lo, q in ((64, g.sync), (80, S), (96, g.sync), (112, S)):
+        q.dma_start(T.raw[lo:lo + 16, 0:1], T.pa[:, :]).then_inc(T.sem.par, 16)
+        if lo == 64:
+            q.dma_start(T.raw[0:64, 0:4], T.de[:, :]).then_inc(T.sem.par, 16)
+    for c in range(4):
+        for hh, q in ((0, g.sync), (1, S)):
+            q.dma_start(T.wo[32 * c + 16 * hh:32 * c + 16 * hh + 16, :], T.x[:, CH * c:CH * c + CH]).then_inc(T.sem.xl, 16)
+
+    imp = {"allow_small_or_imprecise_dtypes": True}
+    i1 = gcomp(g.iota, T.mi[64:128, :], [[0, 4]], 0, 1)
+    gcomp(g.iota, T.itr[64:96, :], [[0, 8], [1, 4]], -1, 0, **imp)
+    i6 = gcomp(g.iota, T.itk[64:96, :], [[0, 2], [4, 4], [0, 4]], -8, 0, **imp)
+    gcomp(g.iota, T.ic[0:64, :], [[8, 2], [0, 16]], 0, 1)
+    i7 = gcomp(g.iota, T.ic[64:128, :], [[8, 2], [0, 16]], 0, 4)
+    gcomp(g.iota, T.ie[0:64, :], [[-16, 4]], 0, 1)
+    i2 = gcomp(g.iota, T.ie[64:128, :], [[-4, 4]], 0, 1)
+    gcomp(g.iota, T.fc[96:128, :], [[16, 8], [128, 8]], 9, 0, **imp)
+    i4 = gcomp(g.iota, T.fn[96:128, :], [[0, 8], [1, 8]], 0, 0, **imp)
+    i5 = gcomp(g.iota, T.jf[0:64, :], [[q0 - q1, 2], [0, 64]], -q0, 1)
+
+    hi = slice(64, 128)
+    ands = Op.bitwise_and
+    o1 = em("V", V.memset(T.ones[:, :], 1.0))
+    vs([i1], T.x17[hi, :], T.mi[hi, 0:1], 17, None, ands)
+    vs([], T.x49[hi, :], T.mi[hi, 0:1], 49, None, ands)
+    xc = vs([], T.x48[hi, :], T.mi[hi, 0:1], 48, None, ands)
+    vs([xc], T.m0[hi, :], T.x17[hi, :], 0, None, Op.is_equal)
+    vs([], T.m1[hi, :], T.x17[hi, :], 16, None, Op.is_equal)
+    b3 = vs([], T.one1[hi, :], T.x49[hi, :], 1, None, Op.is_equal)
+    vs([], T.selr[hi, :], T.x48[hi, :], 48, None, Op.is_equal)
+    b4 = vs([], T.sa[hi, :], T.x49[hi, :], 49, 128.0, Op.is_equal, Op.mult)
+    need("S", b3, i6)
+    em("S", S.activation(T.itr[64:96, :], T.itr[64:96, :], Act.Copy, scale=T.m0[64:96, :]))
+    h1 = em("S", S.activation(T.itk[64:96, :], T.itk[64:96, :], Act.Identity, bias=T.one1[64:96, :], scale=T.m1[64:96, :]))
+    need("S", i4)
+    em("S", S.activation(T.fc[96:128, :], T.fc[96:128, :], Act.Copy, scale=T.m0[96:128, :]))
+    g2 = em("S", S.activation(T.fn[96:128, :], T.fn[96:128, :], Act.Copy, scale=T.m1[96:128, :]))
+    c1 = vs([b4], T.sb[hi, :], T.selr[hi, :], -1.0, T.sa[hi, :], Op.mult, Op.add)
+    h2 = vs([i7], T.ic[:, :], T.ic[:, :], 8, None, ands)
+    c3 = vs([c1], T.sc[hi, :], T.one1[hi, :], -1.0, T.sb[hi, :], Op.mult, Op.add)
+    h4 = vs([h2], T.cm[:, :], T.ic[:, :], 0, None, Op.is_equal)
+    h3 = vt([h1], T.itm[64:96, :], T.itr[64:96, :], T.itk[64:96, :], Op.add)
+    c4 = vs([c3], T.selq[hi, :], T.sc[hi, :], 1.0, None, Op.add)
+    h5 = vt([h3, h4], T.cm[64:96, :], T.cm[64:96, :], T.itm[64:96, :], Op.mult)
+    vs([i2], T.iee[0:64, :], T.ie[0:64, :], 48, None, ands)
+    vs([], T.iee[hi, :], T.ie[hi, :], 13, None, ands)
+    vs([], T.io1[64:96, :], T.ie[64:96, :], 61, None, ands)
+    xf = vs([], T.ie2[96:128, :], T.ie[96:128, :], -3, None, ands)
+
+    V.wait_ge(T.sem.par, 80)
+    vs([], T.hq[hi, :], T.raw[hi, 0:1], 7, None, Op.arith_shift_right)
+    p1 = vs([], T.lr[hi, :], T.raw[hi, 0:1], 127, None, ands)
+    vs([], T.pf[0:64, :], T.raw[0:64, :], 2048.0, None, Op.subtract)
+    p2 = vs([p1, c4], T.a0[hi, :], T.hq[hi, :], T.selq[hi, :], T.one1[hi, :], Op.mult, Op.add)
+    p3 = vs([p2], T.a1[hi, :], T.lr[hi, :], T.selr[hi, :], T.a0[hi, :], Op.mult, Op.add)
+    p4 = vs([p3, o1], T.pf[hi, :], T.ones[hi, :], T.a1[hi, :], None, Op.mult)
+    for c in range(4):
+        l0 = vs([p4, h5], T.l0[:, 32 * c:32 * c + 32], T.cm[:, :], T.pf[:, c:c + 1], None, Op.mult)
+    need("G", l0)
+    nps = [0]
+    came = {}
+    for ds in ((3,), (2, 1)):
+        m = topo.mask(core, peer[ds[0]]) & topo.mask(core, peer[ds[-1]])
+        ne = bin(m).count("1")
+        nps[0] += ne
+        ids, outs = [], []
+        for d in ds:
+            came[4 - d] = ne
+            rid, pid, _se = topo.addr(peer[d])
+            ids.append(DstId(rid=rid, pnc=pid))
+            outs.append(T.lin[:, 128 * (4 - d):128 * (4 - d) + 128])
+        g.remote_dma_fused([RemoteDMATransfer(dst_ids=ids, dma_engine_mask=m, remote_sem=T.sem["pr%d" % k],
+                                              srcs=[T.l0[:, :]], dsts=outs)], local_sem=T.sem.ps)
+    a8 = gcomp(g.iota, T.isel[:, :], [[-1, 32]], 0, 1)
+
+    b5 = vs([xf], T.ea[:, :], T.iee[:, :], 0, 1.0 / 2048, Op.is_equal, Op.mult)
+    vs([], T.oa[64:96, :], T.io1[64:96, :], 1, -1023.5 / 2048, Op.is_equal, Op.mult)
+    vs([], T.ob[64:96, :], T.io1[64:96, :], 1, -127.5 / 256, Op.is_equal, Op.mult)
+    f0 = vs([i5], T.jf[0:64, :], T.jf[0:64, :], 7, None, ands)
+    c2 = vs([b5], T.eb[:, :], T.ea[:, :], 8.0, None, Op.mult)
+    vt([g2], T.f[96:128, 0:64], T.fc[96:128, :], T.fn[96:128, :], Op.add)
+    f2 = vt([], T.f[96:128, 64:128], T.fc[96:128, :], T.fn[96:128, :], Op.add)
+    vt([c2], T.ea[64:96, :], T.ea[64:96, :], T.oa[64:96, :], Op.add)
+    d2 = vt([], T.eb[64:96, :], T.eb[64:96, :], T.ob[64:96, :], Op.add)
+    em("V", V.memset(T.f[64:96, :], 1.0))
+    f1 = vs([f0], T.f[0:64, :], T.jf[0:64, :], 0, 256.0, Op.is_equal, Op.mult)
+    rh = {}
+
+    def right(p):
+        vs([f1, f2, d2], T.rha[:, 128 * p:128 * p + 128], T.f[:, :], T.ea[:, p:p + 1], None, Op.mult)
+        rh[p] = vs([], T.rhb[:, 128 * p:128 * p + 128], T.f[:, :], T.eb[:, p:p + 1], None, Op.mult)
+
+    em("V", V.memset(T.mg[0:1, :], MAGIC))
+    ob = em("V", V.memset(T.onesb[0:1, :], 1.0))
+    right(0)
+    e2 = vs([], T.e2[96:128, :], T.ie2[96:128, :], 49, 1.0 / 4096, Op.is_equal, Op.mult)
+
+    g.wait_ge(T.sem.xl, 128)
+    rid, pid, _se = topo.addr(sib)
+    g.remote_dma(T.ws[:, :], T.wo[:, :], T.sem.xr, T.sem.xs, pid, rid, topo.mask(core, sib))
+    nx = len(topo.engines(core, sib))
+
+    units = [(0, p, 0) for p in range(FIRST)] + [(1, p, 0) for p in range(4)] + [(1, p, 1) for p in range(4)]
+    for d in (2, 3):
+        units += [(d, p, w) for p in range(4) for w in (0, 1)]
+    units += [(0, p, 0) for p in range(FIRST, 4)] + [(0, p, 1) for p in range(4)]
+    at = {u: float(i) for i, u in enumerate(units)}
+    END = float(len(units))
+    LAST = units[-1]
+    items = []
+    tok = {}
+    gat = {u: [] for u in units}
+    use = {n: [] for n in ("A0", "A1", "B0", "B1", "s0", "s1", "xb", "yp")}
+    used = [0, 0]
+    chunkno, chunkof = {}, {}
+
+    def put(key, E, fn, cost=0.0):
+        items.append((key, len(items), E, fn, cost))
+
+    def span(ps):
+        return 128 * ps[0], 128 * ps[-1] + 128
+
+    def chunk(d, ps, keys, first):
+        i = len(chunkno) % 2
+        chunkno[d, ps] = i
+        for p in ps:
+            chunkof[d, p] = ps
+        lo, hi = span(ps)
+        n = hi - lo
+        an, bn = "A%d" % i, "B%d" % i
+        A, B = T[an], T[bn]
+        W, Z, VV, OFF, AS = [T["%s%d" % (nm, d)] for nm in ("w", "z", "v", "off", "as")]
+
+        def times():
+            if d and first:
+                P.wait_ge(T.sem["pr%d" % ((k + d) % 4)], came[d])
+            assert len(use[an]) == len(use[bn]) == used[i]
+            used[i] += 1
+            need("P", l0, rh[ps[-1]], e2, ob, *(use[an] + use[bn]))
+            L = T.lin[:, 128 * d:128 * d + 128] if d else T.l0[:, :]
+            for bank, r in ((A, T.rha), (B, T.rhb)):
+                P.matmul(bank[:, 0:n], L, r[:, lo:hi], True, False)
+                tok[bank is A, d, ps] = em("P", P.matmul(bank[:, 0:n], T.onesb[0:1, :], T.mg[0:1, 0:n], False, True))
+                if first and bank is A:
+                    need("P", *use["yp"])
+                    L2 = T.lin[96:128, 128 * d:128 * d + 128] if d else T.l0[96:128, :]
+                    tok["ap", d] = em("P", P.matmul(T.yp[:, 4 * d:4 * d + 4], L2, T.e2[96:128, :], True, True))
+
+        def squares():
+            need("S", tok[True, d, ps])
+            a = em("S", S.activation(W[:, lo:hi], A[:, 0:n], Act.Square, bias=256.0 - MAGIC))
+            use[an].append(a)
+            if first:
+                need("S", tok["ap", d])
+                tok["as", d] = em("S", S.activation(AS[:, :], T.yp[:, 4 * d:4 * d + 4], Act.Copy))
+                use["yp"].append(tok["as", d])
+            need("S", a, tok["as", d])
+            for p in ps:
+                c = 128 * p
+                tok["z", d, ps] = em("S", S.activation(Z[:, c:c + 128], W[:, c:c + 128], Act.Identity, bias=-HALF, scale=AS[:, p:p + 1]))
+
+        def part0():
+            need("V", tok["z", d, ps], tok[False, d, ps])
+            tok["v", d, ps] = em("V", V.tensor_tensor(VV[:, lo:hi], B[:, 0:n], Z[:, lo:hi], Op.add))
+            use[bn].append(tok["v", d, ps])
+
+        def part1():
+            tok["off", d, ps] = vs([tok["v", d, ps]], OFF[:, lo:hi], VV[:, lo:hi], MAGIC - 2048, None, Op.subtract)
+
+        put(keys[0], "P", times)
+        put(keys[1], "S", squares, 2 * n + 64 * first)
+        put(keys[2], "V", part0, n)
+        put(keys[3], "V", part1, n)
+
+    def ucol(u):
+        return 1024 * units.index(u)
+
+    def gather(u, E, z0, z1):
+        d, p, w = u
+        need_x = ("xr", nx) if w else ("xl", 128)
+        if (need_x, E) not in tok:
+            tok[need_x, E] = 1
+            queue[E].wait_ge(T.sem[need_x[0]], need_x[1])
+        need(E, tok["off", d, chunkof[d, p]])
+        o = 128 * p + 64 * w
+        c = ucol(u)
+        ind = (T.ws if w else T.wo)[:, 0:CH].indirect(T["off%d" % d][:, o + 8 * z0:o + 8 * z1])
+        out = T.gall[:, c + 128 * z0:c + 128 * z1]
+        gat[u].append((z0, z1, em(E, V.tensor_copy(out, ind) if E == "V" else S.activation(out, ind, Act.Copy))))
+
+    sl = {}
+    nsent, nout = [0], [0]
+    nb = [0]
+
+    def summing(bank, ps, d, lazy):
+        B = T[bank]
+        opened = []
+
+        def one(u, z, start, stop):
+            c = ucol(u) + 128 * z
+            c0 = 128 * (u[1] - ps[0]) + 32 * (z % 4)
+            return P.matmul(B[:, c0:c0 + 32], T.gall[:, c:c + 128], (T.sel2 if z > 3 else T.sel1)[:, :], start, stop)
+
+        def whole(p):
+            def fn():
+                need("P", sl[0], *([t for w in (0, 1) for _a, _b, t in gat[d, p, w]] + use[bank]))
+                for z in range(4):
+                    for i, (w, zz) in enumerate(((0, z), (0, z + 4), (1, z), (1, z + 4))):
+                        ins = one((d, p, w), zz, i == 0, i == 3)
+                tok["sum", d, p] = em("P", ins)
+            return fn
+
+        def part(p, w, last):
+            def fn():
+                if not opened:
+                    opened.append(1)
+                    n = 128 * len(ps)
+                    need("P", ob, tok["zer"], *use[bank])
+                    P.matmul(B[:, 0:n], T.onesb[0:1, :], T.zer[0:1, 0:n], True, False)
+                need("P", sl[0])
+                todo = sorted(gat[d, p, w], key=lambda q: (q[0] % 4, q[0]))
+                for i, (z0, z1, t) in enumerate(todo):
+                    need("P", t)
+                    for z in range(z0, z1):
+                        ins = one((d, p, w), z, False, last and i == len(todo) - 1 and z == z1 - 1)
+                tok["sum", d, p] = em("P", ins)
+            return fn
+
+        for p in ps:
+            if not lazy:
+                put(at[d, p, 1] + 0.5, "P", whole(p))
+            else:
+                for w in (0, 1):
+                    put(max(at[d, p, w] + (0.5 if d else 0.4), 21.5 + .01 * p), "P", part(p, w, w == 1 and p == ps[-1]))
+
+    def block(d, j, ps):
+        bank = "s%d" % (nb[0] % 2)
+        nb[0] += 1
+        lo, hi = span(ps)
+        summing(bank, ps, d, d == 3 and j == len(BLOCKS) - 1)
+
+        def evac():
+            need("V", *[tok["sum", d, p] for p in ps])
+            tok["ev", d, j] = em("V", V.tensor_copy(T["snd%d" % d][:, lo:hi], T[bank][:, 0:hi - lo]))
+            use[bank].append(tok["ev", d, j])
+
+        def send():
+            need("G", tok["ev", d, j])
+            rid, pid, _se = topo.addr(peer[d])
+            g.remote_dma(T["rcv%d" % d][:, lo:hi], T["snd%d" % d][:, lo:hi], T.sem["ar%d%d" % (d, j)], T.sem.sent,
+                         pid, rid, topo.mask(core, peer[d]))
+            nsent[0] += len(topo.engines(core, peer[d]))
+
+        key = at[d, ps[-1], 1] + (EVAC3 if d == 3 else EVAC)
+        put(key, "V", evac, 128 * len(ps))
+        put(key, "G", send)
+
+    def unpack(d, j, ps):
+        lo, hi = span(ps)
+
+        def fn():
+            V.wait_ge(T.sem["ar%d%d" % (d, j)], len(topo.engines(peer[4 - d], core)))
+            R = T["rcv%d" % d]
+            if d == 1:
+                t = em("V", V.tensor_copy(T.acc[:, lo:hi], R[:, lo:hi]))
+            else:
+                need("V", *use["xb"])
+                a = em("V", V.tensor_copy(T.xb[:, lo:hi], R[:, lo:hi]))
+                need("V", a, *[tok["acc", p] for p in ps])
+                t = em("V", V.tensor_tensor(T.acc[:, lo:hi], T.acc[:, lo:hi], T.xb[:, lo:hi], Op.add))
+                use["xb"].append(t)
+            for p in ps:
+                tok["acc", p] = t
+        return fn
+
+    def finish(j, ps, bank):
+        lo, hi = span(ps)
+
+        def fn():
+            t = vt([tok["acc", p] for p in ps] + [tok["sum", 0, p] for p in ps],
+                   T.tot[:, lo:hi], T.acc[:, lo:hi], T[bank][:, 0:hi - lo], Op.add)
+            use[bank].append(t)
+            x1 = vs([t], T.ta[:, lo:hi], T.tot[:, lo:hi], 511, None, Op.bitwise_and)
+            x2 = vs([], T.tb[:, lo:hi], T.tot[:, lo:hi], 9, None, Op.arith_shift_right)
+            tok["ca", j] = vs([x1], T.ca[:, lo:hi], T.ta[:, lo:hi], 255, None, Op.min)
+            tok["cb", j] = vs([x2], T.cb[:, lo:hi], T.tb[:, lo:hi], 255, None, Op.min)
+        return fn
+
+    def turn(j, ps, bank):
+        def fn():
+            need("P", sl[0], tok["ca", j], *use[bank])
+            for z in range(8):
+                if z == 4:
+                    need("P", tok["cb", j])
+                for p in ps:
+                    c = 128 * p + 32 * (z % 4)
+                    ins = P.matmul(T[bank][32 * p:32 * p + 32, 16 * z:16 * z + 16], (T.cb if z > 3 else T.ca)[:, c:c + 32],
+                                   T.selb[:, :], True, True)
+            tok["turn", j] = em("P", ins)
+        return fn
+
+    def leave(j, ps, bank):
+        lo, hi = 32 * ps[0], 32 * ps[-1] + 32
+
+        def fn():
+            need("S", tok["turn", j])
+            t = em("S", S.activation(T.ysb[lo:hi, :], T[bank][lo:hi, 0:128], Act.Copy))
+            need("Y", t)
+            g.sync.dma_start(T.y[lo:hi, :], T.ysb[lo:hi, :]).then_inc(T.sem.out, 16)
+            nout[0] += 16
+        return fn
+
+    def later():
+        right(2)
+        right(3)
+        tok["zer"] = em("V", V.memset(T.zer[0:1, :], 0.0))
+
+    def selections():
+        x = vs([a8], T.isel[:, :], T.isel[:, :], 31, None, Op.bitwise_and)
+        y = vs([x], T.isel2[:, :], T.isel[:, 0:16], 15, None, Op.bitwise_and)
+        vs([y], T.selb[:, :], T.isel2[:, :], 0, None, Op.is_equal)
+        vs([], T.sel1[:, :], T.isel[:, :], 0, None, Op.is_equal)
+        sl[0] = vs([], T.sel2[:, :], T.isel[:, :], 0, 512.0, Op.is_equal, Op.mult)
+
+    put(-9.5, "V", lambda: right(1))
+    put(-8.85, "V", later)
+    for i, (ps, keys) in enumerate(OWN_CHUNKS):
+        chunk(0, ps, keys, i == 0)
+    put(3.5, "V", selections, 320)
+    for i, (ps, keys) in enumerate(FIRST_CHUNKS):
+        chunk(1, ps, keys, i == 0)
+    for d in (2, 3):
+        for i, ps in enumerate(BLOCKS):
+            chunk(d, ps, [at[d, ps[0], 0] + c for c in LATER_CHUNKS], i == 0)
+    for d in (1, 2, 3):
+        for j, ps in enumerate(BLOCKS):
+            block(d, j, ps)
+            key = END + 0.01 + 0.09 * j if d == 3 else min(at[d, ps[-1], 1] + 9.2, END - 0.09)
+            put(key, "V", unpack(d, j, ps), 256 * len(ps))
+    for j, ps in enumerate(GROUPS):
+        bank, out = ("A0", "A1", "B0")[j], ("yp", "B1", "s0")[j]
+        summing(bank, ps, 0, True)
+        key = END + 0.05 * (1, 3, 4)[j]
+        put(key, "V", finish(j, ps, bank))
+        put(key + 0.02, "P", turn(j, ps, out))
+        put(key + 0.9, "S", leave(j, ps, out))
+    put(END - 5.01, "V", None, CREDIT)
+    for u in units:
+        put(at[u], "GATHER", u)
+
+    items.sort(key=lambda it: (it[0], it[1]))
+    load = {"V": 0.0, "S": 0.0}
+    for key, _i, E, fn, cost in items:
+        if E == "GATHER":
+            hs = []
+            for h in (0, 1):
+                e = "V" if load["V"] <= load["S"] else "S"
+                load[e] += 512 * KAPPA + 50
+                hs.append(e)
+            if fn == LAST and hs[0] != hs[1]:
+                for z in (0, 2):
+                    gather(fn, hs[0], z, z + 2)
+                    gather(fn, hs[1], 4 + z, 6 + z)
+            elif hs[0] == hs[1]:
+                gather(fn, hs[0], 0, 8)
+            else:
+                gather(fn, hs[0], 0, 4)
+                gather(fn, hs[1], 4, 8)
+            continue
+        if E in load and key >= -0.3:
+            load[E] += cost
+        if fn is not None:
+            fn()
+    g.wait_ge(T.sem.out, nout[0])
+    g.wait_ge(T.sem.ps, nps[0])
+    g.wait_ge(T.sem.xs, nx)
+    g.wait_ge(T.sem.sent, nsent[0])
+    for E in ("V", "S", "P", "G"):
+        need("G", (E, cnt[E]))

@@ -3,54 +3,46 @@ from concourse.mybir import AluOpType as Op, ActivationFunctionType as Act
 
 MAGIC = 12582912.0
 HALF = 2047.5 / 4096.0
+BASE = 1536.0
 CH = 4096
-KAPPA = 1.6
+OWNER = {1: 1, 2: 3, 3: 2}
+ONTO = {1: 2, 2: 3, 3: 2}
 FIRST = 3
-OWN_CHUNKS = (((0,), (-9, -9, -8.998, -8.997)), ((1,), (-8.9, -8.9, -8.898, -8.897)), ((2, 3), (-8.8, 0.2, 1.2, 1.6)))
-FIRST_CHUNKS = (((0, 1), (1.3, 1.8, 2.6, 2.7)), ((2, 3), (1.31, 2.3, 3.6, 4.1)))
-LATER_CHUNKS = (-8.2, -6.8, -5.9, -4.7)
+OWN_CHUNKS = ((0,), (1,), (2, 3))
 BLOCKS = ((0, 1), (2, 3))
 GROUPS = ((0, 1), (2,), (3,))
-EVAC, EVAC3 = 2.7, 1.6
-CREDIT = 3000.0
+PLAN = dict(kappa=1.5, lag=150, own=3500, other=9500, lists=(5500, 9000, 16000), sums=4500, ahead=3.0, behind=2.0, fine=5,
+            reach=4.5)
 
 SCRATCH = {
     "wo": ("sbuf", [128, CH], "bfloat16"), "ws": ("sbuf", [128, CH], "bfloat16"),
-    "raw": ("sbuf", [128, 4], "int32"), "pf": ("sbuf", [128, 4], "float32"), "ones": ("sbuf", [128, 4], "float32"),
-    "hq": ("sbuf", [128, 1], "int32"), "lr": ("sbuf", [128, 1], "int32"),
-    "a0": ("sbuf", [128, 1], "float32"), "a1": ("sbuf", [128, 1], "float32"),
-    "mi": ("sbuf", [128, 4], "int32"), "x17": ("sbuf", [128, 1], "int32"), "x48": ("sbuf", [128, 1], "int32"),
-    "x49": ("sbuf", [128, 1], "int32"), "m0": ("sbuf", [128, 1], "float32"), "m1": ("sbuf", [128, 1], "float32"),
-    "selr": ("sbuf", [128, 1], "float32"), "selq": ("sbuf", [128, 1], "float32"), "one1": ("sbuf", [128, 1], "float32"),
-    "sa": ("sbuf", [128, 1], "float32"), "sb": ("sbuf", [128, 1], "float32"), "sc": ("sbuf", [128, 1], "float32"),
-    "ic": ("sbuf", [128, 32], "int32"), "cm": ("sbuf", [128, 32], "float32"),
-    "itr": ("sbuf", [128, 32], "float32"), "itk": ("sbuf", [128, 32], "float32"), "itm": ("sbuf", [128, 32], "float32"),
-    "ie": ("sbuf", [128, 4], "int32"), "iee": ("sbuf", [128, 4], "int32"), "ie2": ("sbuf", [128, 4], "int32"),
-    "io1": ("sbuf", [128, 4], "int32"), "oa": ("sbuf", [128, 4], "float32"), "ob": ("sbuf", [128, 4], "float32"),
-    "ea": ("sbuf", [128, 4], "float32"), "eb": ("sbuf", [128, 4], "float32"), "e2": ("sbuf", [128, 4], "float16"),
-    "jf": ("sbuf", [128, 128], "int32"), "f": ("sbuf", [128, 128], "float32"),
-    "fc": ("sbuf", [128, 64], "float32"), "fn": ("sbuf", [128, 64], "float32"),
-    "rha": ("sbuf", [128, 512], "float16"), "rhb": ("sbuf", [128, 512], "float16"),
-    "l0": ("sbuf", [128, 128], "float16"), "lin": ("sbuf", [128, 512], "float16"),
-    "mg": ("sbuf", [128, 512], "bfloat16"), "zer": ("sbuf", [128, 256], "bfloat16"),
-    "isel": ("sbuf", [128, 32], "int32"), "sel1": ("sbuf", [128, 32], "bfloat16"), "sel2": ("sbuf", [128, 32], "bfloat16"),
-    "isel2": ("sbuf", [128, 16], "int32"), "selb": ("sbuf", [128, 16], "bfloat16"), "onesb": ("sbuf", [128, 128], "bfloat16"),
+    "raw": ("sbuf", [128, 4], "int32"), "hq": ("sbuf", [128, 1], "int32"), "hf": ("sbuf", [128, 1], "float32"),
+    "pf": ("sbuf", [128, 4], "float32"), "ones": ("sbuf", [128, 64], "float32"),
+    "val": ("sbuf", [128, 64], "int32"), "xm": ("sbuf", [128, 14], "int32"), "e": ("sbuf", [128, 14], "float32"),
+    "p0": ("sbuf", [128, 16], "float32"), "p1": ("sbuf", [128, 16], "float32"), "pat": ("sbuf", [128, 16], "float32"),
+    "cm": ("sbuf", [128, 32], "float32"), "fc": ("sbuf", [128, 64], "float32"), "f": ("sbuf", [128, 128], "float32"),
+    "m": ("sbuf", [128, 1], "float32"), "b1": ("sbuf", [128, 1], "float32"), "b2": ("sbuf", [128, 1], "float32"),
+    "b3": ("sbuf", [128, 1], "float32"), "ec": ("sbuf", [128, 1], "float32"), "e2": ("sbuf", [128, 4], "float16"),
+    "r": ("sbuf", [128, 512], "float16"), "l0": ("sbuf", [128, 128], "float16"), "lin": ("sbuf", [128, 512], "float16"),
+    "row": ("sbuf", [128, 256], "bfloat16"), "ka": ("sbuf", [128, 128], "bfloat16"), "kb": ("sbuf", [128, 128], "bfloat16"),
+    "x31": ("sbuf", [128, 32], "int32"), "x15": ("sbuf", [128, 16], "int32"),
+    "sel1": ("sbuf", [128, 32], "bfloat16"), "sel2": ("sbuf", [128, 32], "bfloat16"),
+    "selV": ("sbuf", [128, 16], "bfloat16"), "selS": ("sbuf", [128, 16], "bfloat16"),
+    "jd": ("sbuf", [128, 128], "int32"), "idp": ("sbuf", [128, 128], "float16"), "idn": ("sbuf", [128, 128], "float16"),
     "gall": ("sbuf", [128, 32768], "bfloat16"),
-    "acc": ("sbuf", [128, 512], "float32"), "tot": ("sbuf", [128, 512], "int32"),
-    "ta": ("sbuf", [128, 512], "int32"), "tb": ("sbuf", [128, 512], "int32"),
-    "ca": ("sbuf", [128, 512], "bfloat16"), "cb": ("sbuf", [128, 512], "bfloat16"),
+    "h2": ("sbuf", [128, 512], "float16"), "h3": ("sbuf", [128, 512], "float16"), "clo": ("sbuf", [128, 512], "bfloat16"), "chi": ("sbuf", [128, 512], "bfloat16"),
     "ysb": ("sbuf", [128, 128], "float32"),
 }
-for _n in ("A0", "A1", "B0", "B1", "s0", "s1", "xb", "yp"):
+for _n in ("L0", "L1", "L2", "L3", "L4", "L5", "s0", "s1"):
     SCRATCH[_n] = ("psum", [128, 512], "float32")
 for _d in range(4):
-    for _n, _t in (("w", "float32"), ("z", "float32"), ("v", "float32"), ("off", "uint16")):
-        SCRATCH["%s%d" % (_n, _d)] = ("sbuf", [128, 512], _t)
+    SCRATCH["w%d" % _d] = ("sbuf", [128, 512], "float32")
+    SCRATCH["off%d" % _d] = ("sbuf", [128, 512], "uint16")
     SCRATCH["as%d" % _d] = ("sbuf", [128, 4], "float32")
     if _d:
         SCRATCH["snd%d" % _d] = ("sbuf", [128, 512], "uint16")
         SCRATCH["rcv%d" % _d] = ("sbuf", [128, 512], "uint16")
-SEMAPHORES = ["V", "S", "P", "G", "par", "xl", "xs", "xr", "ps", "out", "sent"] + ["pr%d" % k for k in range(4)] \
+SEMAPHORES = ["V", "S", "P", "G", "par", "xl", "xs", "xr", "ps", "out", "sent"] + ["pr%d" % d for d in range(4)] \
     + ["ar%d%d" % (d, b) for d in range(1, 4) for b in range(len(BLOCKS))]
 
 
@@ -63,12 +55,15 @@ def rank_program(g, core, T, topo):
     for c in cores:
         if topo.chip(c) not in chips:
             chips.append(topo.chip(c))
+    ca = chips[0]
+    cb = [c for c in chips[1:] if not topo.same_plane(ca, c)][0]
+    chips = [ca, cb] + [[c for c in chips if topo.same_plane(x, c)][0] for x in (ca, cb)]
     on = [[c for c in cores if topo.chip(c) == ch] for ch in chips]
     k = chips.index(topo.chip(core))
     pos = on[k].index(core)
     sib = [c for c in on[k] if c != core][0]
-    q0, q1 = me, T.rank_of(sib)
-    peer = [on[(k + d) % 4][pos] for d in range(4)]
+    qs = (me, T.rank_of(sib))
+    peer = [on[k ^ x][pos] for x in range(4)]
 
     V, S, P = g.vector, g.scalar, g.tensor
     queue = {"V": V, "S": S, "P": P, "G": g, "Y": g.sync}
@@ -90,393 +85,428 @@ def rank_program(g, core, T, topo):
                 queue[E].wait_ge(T.sem[s], best[s])
                 seen[(E, s)] = best[s]
 
-    def gcomp(fn, *a, **kw):
-        need("G", ("G", cnt["G"]))
-        return em("G", fn(*a, **kw))
-
     def vs(needs, out, in0, s1, s2, op0, op1=None):
         need("V", *needs)
         if op1 is None:
             return em("V", V.tensor_scalar(out, in0, s1, None, op0))
         return em("V", V.tensor_scalar(out, in0, s1, s2, op0, op1))
 
-    def vt(needs, out, in0, in1, op):
-        need("V", *needs)
-        return em("V", V.tensor_tensor(out, in0, in1, op))
+    def sa(needs, out, in_, func=Act.Identity, **kw):
+        need("S", *needs)
+        return em("S", S.activation(out, in_, func, **kw))
 
-    for lo, q in ((64, g.sync), (80, S), (96, g.sync), (112, S)):
-        q.dma_start(T.raw[lo:lo + 16, 0:1], T.pa[:, :]).then_inc(T.sem.par, 16)
-        if lo == 64:
-            q.dma_start(T.raw[0:64, 0:4], T.de[:, :]).then_inc(T.sem.par, 16)
+    def dst(c):
+        rid, pid, _se = topo.addr(c)
+        return DstId(rid=rid, pnc=pid)
+
+    lo, hi = slice(0, 64), slice(64, 128)
+    ands, eq, mul, add = Op.bitwise_and, Op.is_equal, Op.mult, Op.add
+
+    one = em("V", V.memset(T.raw[96:128, :], 1))
+    g.sync.dma_start(T.raw[lo, 0:4], T.de[:, :]).then_inc(T.sem.par, 16)
+    for s in range(6):
+        E = "YS"[s % 2]
+        if s > 3:
+            need(E, one)
+        c = 0 if s in (3, 5) else 1
+        queue[E].dma_start(T.raw[64 + 8 * s:72 + 8 * s, c:c + 2], T.pa[:, :]).then_inc(T.sem.par, 16)
     for c in range(4):
         for hh, q in ((0, g.sync), (1, S)):
             q.dma_start(T.wo[32 * c + 16 * hh:32 * c + 16 * hh + 16, :], T.x[:, CH * c:CH * c + CH]).then_inc(T.sem.xl, 16)
 
     imp = {"allow_small_or_imprecise_dtypes": True}
-    i1 = gcomp(g.iota, T.mi[64:128, :], [[0, 4]], 0, 1)
-    gcomp(g.iota, T.itr[64:96, :], [[0, 8], [1, 4]], -1, 0, **imp)
-    i6 = gcomp(g.iota, T.itk[64:96, :], [[0, 2], [4, 4], [0, 4]], -8, 0, **imp)
-    gcomp(g.iota, T.ic[0:64, :], [[8, 2], [0, 16]], 0, 1)
-    i7 = gcomp(g.iota, T.ic[64:128, :], [[8, 2], [0, 16]], 0, 4)
-    gcomp(g.iota, T.ie[0:64, :], [[-16, 4]], 0, 1)
-    i2 = gcomp(g.iota, T.ie[64:128, :], [[-4, 4]], 0, 1)
-    gcomp(g.iota, T.fc[96:128, :], [[16, 8], [128, 8]], 9, 0, **imp)
-    i4 = gcomp(g.iota, T.fn[96:128, :], [[0, 8], [1, 8]], 0, 0, **imp)
-    i5 = gcomp(g.iota, T.jf[0:64, :], [[q0 - q1, 2], [0, 64]], -q0, 1)
-
-    hi = slice(64, 128)
-    ands = Op.bitwise_and
+    i1 = em("G", g.iota(T.val[:, :], [[-1, 64]], 0, 1))
+    need("G", i1)
+    i2 = em("G", g.iota(T.p0[64:96, :], [[0, 4], [1, 4]], -2, 0, **imp))
+    em("G", g.iota(T.fc[96:128, :], [[0, 8], [1, 8]], 0, 0, **imp))
+    need("G", i2)
+    i2 = em("G", g.iota(T.p1[64:96, :], [[4, 4], [0, 4]], -9, 0, **imp))
+    need("G", i2)
+    i3 = em("G", g.iota(T.fc[64:96, :], [[16, 8], [128, 8]], 9, 0, **imp))
     o1 = em("V", V.memset(T.ones[:, :], 1.0))
-    vs([i1], T.x17[hi, :], T.mi[hi, 0:1], 17, None, ands)
-    vs([], T.x49[hi, :], T.mi[hi, 0:1], 49, None, ands)
-    xc = vs([], T.x48[hi, :], T.mi[hi, 0:1], 48, None, ands)
-    vs([xc], T.m0[hi, :], T.x17[hi, :], 0, None, Op.is_equal)
-    vs([], T.m1[hi, :], T.x17[hi, :], 16, None, Op.is_equal)
-    b3 = vs([], T.one1[hi, :], T.x49[hi, :], 1, None, Op.is_equal)
-    vs([], T.selr[hi, :], T.x48[hi, :], 48, None, Op.is_equal)
-    b4 = vs([], T.sa[hi, :], T.x49[hi, :], 49, 128.0, Op.is_equal, Op.mult)
-    need("S", b3, i6)
-    em("S", S.activation(T.itr[64:96, :], T.itr[64:96, :], Act.Copy, scale=T.m0[64:96, :]))
-    h1 = em("S", S.activation(T.itk[64:96, :], T.itk[64:96, :], Act.Identity, bias=T.one1[64:96, :], scale=T.m1[64:96, :]))
-    need("S", i4)
-    em("S", S.activation(T.fc[96:128, :], T.fc[96:128, :], Act.Copy, scale=T.m0[96:128, :]))
-    g2 = em("S", S.activation(T.fn[96:128, :], T.fn[96:128, :], Act.Copy, scale=T.m1[96:128, :]))
-    c1 = vs([b4], T.sb[hi, :], T.selr[hi, :], -1.0, T.sa[hi, :], Op.mult, Op.add)
-    h2 = vs([i7], T.ic[:, :], T.ic[:, :], 8, None, ands)
-    c3 = vs([c1], T.sc[hi, :], T.one1[hi, :], -1.0, T.sb[hi, :], Op.mult, Op.add)
-    h4 = vs([h2], T.cm[:, :], T.ic[:, :], 0, None, Op.is_equal)
-    h3 = vt([h1], T.itm[64:96, :], T.itr[64:96, :], T.itk[64:96, :], Op.add)
-    c4 = vs([c3], T.selq[hi, :], T.sc[hi, :], 1.0, None, Op.add)
-    h5 = vt([h3, h4], T.cm[64:96, :], T.cm[64:96, :], T.itm[64:96, :], Op.mult)
-    vs([i2], T.iee[0:64, :], T.ie[0:64, :], 48, None, ands)
-    vs([], T.iee[hi, :], T.ie[hi, :], 13, None, ands)
-    vs([], T.io1[64:96, :], T.ie[64:96, :], 61, None, ands)
-    xf = vs([], T.ie2[96:128, :], T.ie[96:128, :], -3, None, ands)
+    em("V", V.memset(T.pat[:, :], 1.0))
+    em("V", V.memset(T.row[0:1, :], 1.0))
+    for j, (kk, v) in enumerate(((T.ka, 8 * MAGIC), (T.kb, MAGIC))):
+        for h in (0, 1):
+            kc = sa([o1], kk[0:1, 64 * h:64 * h + 64], T.ones[0:1, :], scale=v)
+    for rows, parts in ((lo, ((64, 16, 48), (16, 8, 8), (8, 1, 7))), (hi, ((8, 2, 6), (2, 1, 1), (64, 8, 56)))):
+        for (c0, c1), (end, step, bits) in zip(((0, 4), (4, 6), (6, 14)), parts):
+            x = vs([i1], T.xm[rows, c0:c1], T.val[rows, 0:end:step], bits, None, ands)
+    e = vs([x], T.e[:, :], T.xm[:, :], 0, None, eq)
 
-    V.wait_ge(T.sem.par, 80)
-    vs([], T.hq[hi, :], T.raw[hi, 0:1], 7, None, Op.arith_shift_right)
-    p1 = vs([], T.lr[hi, :], T.raw[hi, 0:1], 127, None, ands)
-    vs([], T.pf[0:64, :], T.raw[0:64, :], 2048.0, None, Op.subtract)
-    p2 = vs([p1, c4], T.a0[hi, :], T.hq[hi, :], T.selq[hi, :], T.one1[hi, :], Op.mult, Op.add)
-    p3 = vs([p2], T.a1[hi, :], T.lr[hi, :], T.selr[hi, :], T.a0[hi, :], Op.mult, Op.add)
-    p4 = vs([p3, o1], T.pf[hi, :], T.ones[hi, :], T.a1[hi, :], None, Op.mult)
-    for c in range(4):
-        l0 = vs([p4, h5], T.l0[:, 32 * c:32 * c + 32], T.cm[:, :], T.pf[:, c:c + 1], None, Op.mult)
-    need("G", l0)
-    nps = [0]
-    came = {}
-    for ds in ((3,), (2, 1)):
-        m = topo.mask(core, peer[ds[0]]) & topo.mask(core, peer[ds[-1]])
-        ne = bin(m).count("1")
-        nps[0] += ne
-        ids, outs = [], []
-        for d in ds:
-            came[4 - d] = ne
-            rid, pid, _se = topo.addr(peer[d])
-            ids.append(DstId(rid=rid, pnc=pid))
-            outs.append(T.lin[:, 128 * (4 - d):128 * (4 - d) + 128])
-        g.remote_dma_fused([RemoteDMATransfer(dst_ids=ids, dma_engine_mask=m, remote_sem=T.sem["pr%d" % k],
-                                              srcs=[T.l0[:, :]], dsts=outs)], local_sem=T.sem.ps)
-    a8 = gcomp(g.iota, T.isel[:, :], [[-1, 32]], 0, 1)
+    def st(s, rows=hi):
+        return T.e[rows, 6 + s:7 + s]
 
-    b5 = vs([xf], T.ea[:, :], T.iee[:, :], 0, 1.0 / 2048, Op.is_equal, Op.mult)
-    vs([], T.oa[64:96, :], T.io1[64:96, :], 1, -1023.5 / 2048, Op.is_equal, Op.mult)
-    vs([], T.ob[64:96, :], T.io1[64:96, :], 1, -127.5 / 256, Op.is_equal, Op.mult)
-    f0 = vs([i5], T.jf[0:64, :], T.jf[0:64, :], 7, None, ands)
-    c2 = vs([b5], T.eb[:, :], T.ea[:, :], 8.0, None, Op.mult)
-    vt([g2], T.f[96:128, 0:64], T.fc[96:128, :], T.fn[96:128, :], Op.add)
-    f2 = vt([], T.f[96:128, 64:128], T.fc[96:128, :], T.fn[96:128, :], Op.add)
-    vt([c2], T.ea[64:96, :], T.ea[64:96, :], T.oa[64:96, :], Op.add)
-    d2 = vt([], T.eb[64:96, :], T.eb[64:96, :], T.ob[64:96, :], Op.add)
-    em("V", V.memset(T.f[64:96, :], 1.0))
-    f1 = vs([f0], T.f[0:64, :], T.jf[0:64, :], 0, 256.0, Op.is_equal, Op.mult)
+    q64 = slice(64, 96)
+    sa([e, i2], T.p0[q64, :], T.p0[q64, :], scale=st(1, q64), bias=1.0)
+    t2 = sa([], T.p1[q64, :], T.p1[q64, :], scale=st(2, q64))
+    vs([e], T.m[hi, :], st(0), st(4), 1.0 / 256, add, mul)
+    b1 = vs([], T.b1[hi, :], st(1), st(2), 1.0 / 256, add, mul)
+    ec = vs([], T.ec[hi, :], st(3), 128.0, st(5), mul, add)
+    b2 = sa([b1], T.b2[hi, :], st(6), scale=-127.5 / 256, bias=T.b1[hi, :])
+    for w in (0, 1):
+        sa([], T.f[lo, 64 * w:64 * w + 64], T.ones[lo, :], scale=st(qs[w], lo))
+    b3 = sa([b2], T.b3[hi, :], st(7), scale=-3.5, bias=T.b2[hi, :])
+    for w in (0, 1):
+        f = sa([b3, i3], T.f[hi, 64 * w:64 * w + 64], T.fc[hi, :], scale=T.m[hi, :], bias=T.b3[hi, :])
+    need("V", t2)
+    pat = em("V", V.tensor_tensor(T.pat[q64, :], T.p0[q64, :], T.p1[q64, :], add))
+    e2 = vs([ec], T.e2[hi, :], T.e[hi, 0:4], T.ec[hi, :], 1.0 / 4096, mul, mul)
+    for hh in (0, 1):
+        cm = vs([pat], T.cm[:, 16 * hh:16 * hh + 16], T.pat[:, :], T.e[:, 4 + hh:5 + hh], None, mul)
+
     rh = {}
 
     def right(p):
-        vs([f1, f2, d2], T.rha[:, 128 * p:128 * p + 128], T.f[:, :], T.ea[:, p:p + 1], None, Op.mult)
-        rh[p] = vs([], T.rhb[:, 128 * p:128 * p + 128], T.f[:, :], T.eb[:, p:p + 1], None, Op.mult)
+        rh[p] = vs([f], T.r[:, 128 * p:128 * p + 128], T.f[:, :], T.e[:, p:p + 1], None, mul)
+        return rh[p]
 
-    em("V", V.memset(T.mg[0:1, :], MAGIC))
-    ob = em("V", V.memset(T.onesb[0:1, :], 1.0))
+    V.wait_ge(T.sem.par, 16 * 7)
+    vs([], T.hq[q64, :], T.raw[q64, 1:2], 7, None, Op.arith_shift_right)
+    p1 = vs([], T.hq[96:128, :], T.raw[96:128, 1:2], 127, None, ands)
+    vs([], T.pf[lo, :], T.raw[lo, :], 2048.0, None, Op.subtract)
+    need("V", p1)
+    p2 = em("V", V.tensor_copy(T.hf[hi, :], T.hq[hi, :]))
     right(0)
-    e2 = vs([], T.e2[96:128, :], T.ie2[96:128, :], 49, 1.0 / 4096, Op.is_equal, Op.mult)
+    p3 = vs([p2], T.pf[hi, :], T.ones[hi, 0:4], T.hf[hi, :], None, mul)
+    for c in range(4):
+        l0 = vs([p3, cm], T.l0[:, 32 * c:32 * c + 32], T.cm[:, :], T.pf[:, c:c + 1], None, mul)
+    need("G", l0)
+    nps = [0]
+    came = {}
+    for ds in ((1,), (2, 3)):
+        m = topo.mask(core, peer[OWNER[ds[0]]]) & topo.mask(core, peer[OWNER[ds[-1]]])
+        ne = bin(m).count("1")
+        nps[0] += ne
+        came.update({d: ne for d in ds})
+        g.remote_dma_fused([RemoteDMATransfer(dst_ids=[dst(peer[OWNER[d]]) for d in ds], dma_engine_mask=m,
+                                              remote_sem=T.sem["pr%d" % k], srcs=[T.l0[:, :]],
+                                              dsts=[T.lin[:, 128 * d:128 * d + 128] for d in ds])], local_sem=T.sem.ps)
+    need("G", i3)
+    jd = em("G", g.iota(T.jd[:, :], [[-1, 128]], 0, 1))
 
     g.wait_ge(T.sem.xl, 128)
     rid, pid, _se = topo.addr(sib)
     g.remote_dma(T.ws[:, :], T.wo[:, :], T.sem.xr, T.sem.xs, pid, rid, topo.mask(core, sib))
     nx = len(topo.engines(core, sib))
 
-    units = [(0, p, 0) for p in range(FIRST)] + [(1, p, 0) for p in range(4)] + [(1, p, 1) for p in range(4)]
-    for d in (2, 3):
-        units += [(d, p, w) for p in range(4) for w in (0, 1)]
-    units += [(0, p, 0) for p in range(FIRST, 4)] + [(0, p, 1) for p in range(4)]
-    at = {u: float(i) for i, u in enumerate(units)}
-    END = float(len(units))
-    LAST = units[-1]
-    items = []
+    tasks = {}
     tok = {}
-    gat = {u: [] for u in units}
-    use = {n: [] for n in ("A0", "A1", "B0", "B1", "s0", "s1", "xb", "yp")}
-    used = [0, 0]
-    chunkno, chunkof = {}, {}
 
-    def put(key, E, fn, cost=0.0):
-        items.append((key, len(items), E, fn, cost))
+    def task(name, on_, cost, deps, fn, rel=0.0, prio=-1.0):
+        tasks[name] = dict(on=on_, cost=cost, deps=list(deps), fn=fn, rel=rel, prio=prio)
+
+    def toks(names):
+        return [tok[n] for n in names]
 
     def span(ps):
         return 128 * ps[0], 128 * ps[-1] + 128
 
-    def chunk(d, ps, keys, first):
-        i = len(chunkno) % 2
-        chunkno[d, ps] = i
-        for p in ps:
-            chunkof[d, p] = ps
-        lo, hi = span(ps)
-        n = hi - lo
-        an, bn = "A%d" % i, "B%d" % i
-        A, B = T[an], T[bn]
-        W, Z, VV, OFF, AS = [T["%s%d" % (nm, d)] for nm in ("w", "z", "v", "off", "as")]
+    def selections(E):
+        vs([], T.x31[:, :], T.val[:, 0:32], 31, None, ands)
+        x = vs([], T.x15[:, :], T.val[:, 0:16], 15, None, ands)
+        vs([x], T.sel1[:, :], T.x31[:, :], 0, None, eq)
+        vs([], T.sel2[:, :], T.x31[:, :], 0, 256.0, eq, mul)
+        vs([], T.selV[:, :], T.x15[:, :], 0, None, eq)
+        return vs([], T.selS[:, :], T.x15[:, :], 0, -1.0, eq, mul)
 
-        def times():
-            if d and first:
-                P.wait_ge(T.sem["pr%d" % ((k + d) % 4)], came[d])
-            assert len(use[an]) == len(use[bn]) == used[i]
-            used[i] += 1
-            need("P", l0, rh[ps[-1]], e2, ob, *(use[an] + use[bn]))
-            L = T.lin[:, 128 * d:128 * d + 128] if d else T.l0[:, :]
-            for bank, r in ((A, T.rha), (B, T.rhb)):
-                P.matmul(bank[:, 0:n], L, r[:, lo:hi], True, False)
-                tok[bank is A, d, ps] = em("P", P.matmul(bank[:, 0:n], T.onesb[0:1, :], T.mg[0:1, 0:n], False, True))
-                if first and bank is A:
-                    need("P", *use["yp"])
-                    L2 = T.lin[96:128, 128 * d:128 * d + 128] if d else T.l0[96:128, :]
-                    tok["ap", d] = em("P", P.matmul(T.yp[:, 4 * d:4 * d + 4], L2, T.e2[96:128, :], True, True))
+    def identities(E):
+        vs([jd], T.idp[:, :], T.jd[:, :], 0, None, eq)
+        return vs([], T.idn[:, :], T.jd[:, :], 0, -256.0, eq, mul)
 
-        def squares():
-            need("S", tok[True, d, ps])
-            a = em("S", S.activation(W[:, lo:hi], A[:, 0:n], Act.Square, bias=256.0 - MAGIC))
-            use[an].append(a)
+    tok["r", 0] = rh[0]
+    for p in (1, 2, 3):
+        task(("r", p), "V", 150, [], lambda E, p=p: right(p), prio=-9 + p)
+    task("sel", "V", 600, [], selections, prio=-2)
+    task("id", "V", 300, [], identities, rel=1500, prio=-2)
+
+    chunks = [(0, ps) for ps in OWN_CHUNKS] + [(d, ps) for d in (1, 2, 3) for ps in BLOCKS]
+    listof = {}
+
+    def chunk(i, d, ps):
+        first = ps[0] == 0
+        c0, c1 = span(ps)
+        n = c1 - c0
+        A, B = T["L%d" % (2 * i % 6)], T["L%d" % (2 * i % 6 + 1)]
+        W, OFF, AS = [T["%s%d" % (nm, d)] for nm in ("w", "off", "as")]
+        L = T.lin if d else T.l0
+        before = [("off", i - 3)] if i >= 3 else []
+        rs = [("r", p) for p in ps]
+
+        def eighths(E):
+            if d:
+                need("P", ("pr%d" % (k ^ OWNER[d]), came[d]))
+            need("P", l0, e2, kc, *toks(rs + before))
             if first:
-                need("S", tok["ap", d])
-                tok["as", d] = em("S", S.activation(AS[:, :], T.yp[:, 4 * d:4 * d + 4], Act.Copy))
-                use["yp"].append(tok["as", d])
-            need("S", a, tok["as", d])
+                P.matmul(A[:, 256:260], L[hi, 128 * d:128 * d + 128], T.e2[hi, :], True, True)
+            P.matmul(A[:, 0:n], L[:, 128 * d:128 * d + 128], T.r[:, c0:c1], True, False)
+            tok["j", i] = em("P", P.matmul(A[:, 0:n], T.ka[0:1, :], T.row[0:1, 0:n], False, True))
+            return em("P", P.matmul(B[:, 0:n], T.kb[0:1, :], T.row[0:1, 0:n], True, False))
+
+        def bend(E):
+            t = sa([tok["j", i]], W[:, c0:c1], A[:, 0:n], Act.Square, scale=0.125, bias=256.0 - MAGIC)
+            if first:
+                t = tok["as", d] = sa([], AS[:, :], A[:, 256:260], Act.Copy)
+            need("S", tok["a", i])
+            need("S", t)
             for p in ps:
                 c = 128 * p
-                tok["z", d, ps] = em("S", S.activation(Z[:, c:c + 128], W[:, c:c + 128], Act.Identity, bias=-HALF, scale=AS[:, p:p + 1]))
+                t = sa([tok["as", d]], B[:, c - c0:c - c0 + 128], W[:, c:c + 128], bias=-HALF, scale=AS[:, p:p + 1])
+            return t
 
-        def part0():
-            need("V", tok["z", d, ps], tok[False, d, ps])
-            tok["v", d, ps] = em("V", V.tensor_tensor(VV[:, lo:hi], B[:, 0:n], Z[:, lo:hi], Op.add))
-            use[bn].append(tok["v", d, ps])
+        def times(E):
+            need("P", tok["z", i])
+            P.matmul(B[:, 0:n], T.kb[0:1, :], T.row[0:1, 0:n], False, False)
+            return em("P", P.matmul(B[:, 0:n], L[0:120, 128 * d:128 * d + 128], T.r[0:120, c0:c1], False, True))
 
-        def part1():
-            tok["off", d, ps] = vs([tok["v", d, ps]], OFF[:, lo:hi], VV[:, lo:hi], MAGIC - 2048, None, Op.subtract)
+        def places(E):
+            return vs([tok["t", i]], OFF[:, c0:c1], B[:, 0:n], MAGIC - 2048, None, Op.subtract)
 
-        put(keys[0], "P", times)
-        put(keys[1], "S", squares, 2 * n + 64 * first)
-        put(keys[2], "V", part0, n)
-        put(keys[3], "V", part1, n)
-
-    def ucol(u):
-        return 1024 * units.index(u)
-
-    def gather(u, E, z0, z1):
-        d, p, w = u
-        need_x = ("xr", nx) if w else ("xl", 128)
-        if (need_x, E) not in tok:
-            tok[need_x, E] = 1
-            queue[E].wait_ge(T.sem[need_x[0]], need_x[1])
-        need(E, tok["off", d, chunkof[d, p]])
-        o = 128 * p + 64 * w
-        c = ucol(u)
-        ind = (T.ws if w else T.wo)[:, 0:CH].indirect(T["off%d" % d][:, o + 8 * z0:o + 8 * z1])
-        out = T.gall[:, c + 128 * z0:c + 128 * z1]
-        gat[u].append((z0, z1, em(E, V.tensor_copy(out, ind) if E == "V" else S.activation(out, ind, Act.Copy))))
-
-    sl = {}
-    nsent, nout = [0], [0]
-    nb = [0]
-
-    def summing(bank, ps, d, lazy):
-        B = T[bank]
-        opened = []
-
-        def one(u, z, start, stop):
-            c = ucol(u) + 128 * z
-            c0 = 128 * (u[1] - ps[0]) + 32 * (z % 4)
-            return P.matmul(B[:, c0:c0 + 32], T.gall[:, c:c + 128], (T.sel2 if z > 3 else T.sel1)[:, :], start, stop)
-
-        def whole(p):
-            def fn():
-                need("P", sl[0], *([t for w in (0, 1) for _a, _b, t in gat[d, p, w]] + use[bank]))
-                for z in range(4):
-                    for i, (w, zz) in enumerate(((0, z), (0, z + 4), (1, z), (1, z + 4))):
-                        ins = one((d, p, w), zz, i == 0, i == 3)
-                tok["sum", d, p] = em("P", ins)
-            return fn
-
-        def part(p, w, last):
-            def fn():
-                if not opened:
-                    opened.append(1)
-                    n = 128 * len(ps)
-                    need("P", ob, tok["zer"], *use[bank])
-                    P.matmul(B[:, 0:n], T.onesb[0:1, :], T.zer[0:1, 0:n], True, False)
-                need("P", sl[0])
-                todo = sorted(gat[d, p, w], key=lambda q: (q[0] % 4, q[0]))
-                for i, (z0, z1, t) in enumerate(todo):
-                    need("P", t)
-                    for z in range(z0, z1):
-                        ins = one((d, p, w), z, False, last and i == len(todo) - 1 and z == z1 - 1)
-                tok["sum", d, p] = em("P", ins)
-            return fn
-
+        order = [("a", i - 1)] if i else []
+        task(("a", i), "P", 3 * n + 64 * first, before + order + [x for x in rs if x in tasks], eighths,
+             rel=PLAN["lists"][d - 1] if d else 0.0, prio=-5)
+        task(("z", i), "S", 2 * n + 200 + 110 * first, [("a", i)] + ([("z", i - 1)] if i else []), bend, prio=-5)
+        task(("t", i), "P", 2 * n, [("z", i)], times, prio=-6)
+        task(("off", i), "V", n + 25, [("t", i)], places, prio=-10)
         for p in ps:
-            if not lazy:
-                put(at[d, p, 1] + 0.5, "P", whole(p))
-            else:
-                for w in (0, 1):
-                    put(max(at[d, p, w] + (0.5 if d else 0.4), 21.5 + .01 * p), "P", part(p, w, w == 1 and p == ps[-1]))
+            listof[d, p] = i
 
-    def block(d, j, ps):
-        bank = "s%d" % (nb[0] % 2)
-        nb[0] += 1
-        lo, hi = span(ps)
-        summing(bank, ps, d, d == 3 and j == len(BLOCKS) - 1)
+    for i, (d, ps) in enumerate(chunks):
+        chunk(i, d, ps)
 
-        def evac():
-            need("V", *[tok["sum", d, p] for p in ps])
-            tok["ev", d, j] = em("V", V.tensor_copy(T["snd%d" % d][:, lo:hi], T[bank][:, 0:hi - lo]))
-            use[bank].append(tok["ev", d, j])
-
-        def send():
-            need("G", tok["ev", d, j])
-            rid, pid, _se = topo.addr(peer[d])
-            g.remote_dma(T["rcv%d" % d][:, lo:hi], T["snd%d" % d][:, lo:hi], T.sem["ar%d%d" % (d, j)], T.sem.sent,
-                         pid, rid, topo.mask(core, peer[d]))
-            nsent[0] += len(topo.engines(core, peer[d]))
-
-        key = at[d, ps[-1], 1] + (EVAC3 if d == 3 else EVAC)
-        put(key, "V", evac, 128 * len(ps))
-        put(key, "G", send)
-
-    def unpack(d, j, ps):
-        lo, hi = span(ps)
-
-        def fn():
-            V.wait_ge(T.sem["ar%d%d" % (d, j)], len(topo.engines(peer[4 - d], core)))
-            R = T["rcv%d" % d]
-            if d == 1:
-                t = em("V", V.tensor_copy(T.acc[:, lo:hi], R[:, lo:hi]))
-            else:
-                need("V", *use["xb"])
-                a = em("V", V.tensor_copy(T.xb[:, lo:hi], R[:, lo:hi]))
-                need("V", a, *[tok["acc", p] for p in ps])
-                t = em("V", V.tensor_tensor(T.acc[:, lo:hi], T.acc[:, lo:hi], T.xb[:, lo:hi], Op.add))
-                use["xb"].append(t)
-            for p in ps:
-                tok["acc", p] = t
-        return fn
-
-    def finish(j, ps, bank):
-        lo, hi = span(ps)
-
-        def fn():
-            t = vt([tok["acc", p] for p in ps] + [tok["sum", 0, p] for p in ps],
-                   T.tot[:, lo:hi], T.acc[:, lo:hi], T[bank][:, 0:hi - lo], Op.add)
-            use[bank].append(t)
-            x1 = vs([t], T.ta[:, lo:hi], T.tot[:, lo:hi], 511, None, Op.bitwise_and)
-            x2 = vs([], T.tb[:, lo:hi], T.tot[:, lo:hi], 9, None, Op.arith_shift_right)
-            tok["ca", j] = vs([x1], T.ca[:, lo:hi], T.ta[:, lo:hi], 255, None, Op.min)
-            tok["cb", j] = vs([x2], T.cb[:, lo:hi], T.tb[:, lo:hi], 255, None, Op.min)
-        return fn
-
-    def turn(j, ps, bank):
-        def fn():
-            need("P", sl[0], tok["ca", j], *use[bank])
-            for z in range(8):
-                if z == 4:
-                    need("P", tok["cb", j])
-                for p in ps:
-                    c = 128 * p + 32 * (z % 4)
-                    ins = P.matmul(T[bank][32 * p:32 * p + 32, 16 * z:16 * z + 16], (T.cb if z > 3 else T.ca)[:, c:c + 32],
-                                   T.selb[:, :], True, True)
-            tok["turn", j] = em("P", ins)
-        return fn
-
-    def leave(j, ps, bank):
-        lo, hi = 32 * ps[0], 32 * ps[-1] + 32
-
-        def fn():
-            need("S", tok["turn", j])
-            t = em("S", S.activation(T.ysb[lo:hi, :], T[bank][lo:hi, 0:128], Act.Copy))
-            need("Y", t)
-            g.sync.dma_start(T.y[lo:hi, :], T.ysb[lo:hi, :]).then_inc(T.sem.out, 16)
-            nout[0] += 16
-        return fn
-
-    def later():
-        right(2)
-        right(3)
-        tok["zer"] = em("V", V.memset(T.zer[0:1, :], 0.0))
-
-    def selections():
-        x = vs([a8], T.isel[:, :], T.isel[:, :], 31, None, Op.bitwise_and)
-        y = vs([x], T.isel2[:, :], T.isel[:, 0:16], 15, None, Op.bitwise_and)
-        vs([y], T.selb[:, :], T.isel2[:, :], 0, None, Op.is_equal)
-        vs([], T.sel1[:, :], T.isel[:, :], 0, None, Op.is_equal)
-        sl[0] = vs([], T.sel2[:, :], T.isel[:, :], 0, 512.0, Op.is_equal, Op.mult)
-
-    put(-9.5, "V", lambda: right(1))
-    put(-8.85, "V", later)
-    for i, (ps, keys) in enumerate(OWN_CHUNKS):
-        chunk(0, ps, keys, i == 0)
-    put(3.5, "V", selections, 320)
-    for i, (ps, keys) in enumerate(FIRST_CHUNKS):
-        chunk(1, ps, keys, i == 0)
+    units = [(0, p, 0) for p in range(FIRST)] + [(1, p, 0) for p in range(4)] + [(1, p, 1) for p in range(4)]
     for d in (2, 3):
-        for i, ps in enumerate(BLOCKS):
-            chunk(d, ps, [at[d, ps[0], 0] + c for c in LATER_CHUNKS], i == 0)
-    for d in (1, 2, 3):
-        for j, ps in enumerate(BLOCKS):
-            block(d, j, ps)
-            key = END + 0.01 + 0.09 * j if d == 3 else min(at[d, ps[-1], 1] + 9.2, END - 0.09)
-            put(key, "V", unpack(d, j, ps), 256 * len(ps))
-    for j, ps in enumerate(GROUPS):
-        bank, out = ("A0", "A1", "B0")[j], ("yp", "B1", "s0")[j]
-        summing(bank, ps, 0, True)
-        key = END + 0.05 * (1, 3, 4)[j]
-        put(key, "V", finish(j, ps, bank))
-        put(key + 0.02, "P", turn(j, ps, out))
-        put(key + 0.9, "S", leave(j, ps, out))
-    put(END - 5.01, "V", None, CREDIT)
-    for u in units:
-        put(at[u], "GATHER", u)
+        units += [(d, p, w) for p in range(4) for w in (0, 1)]
+    units += [(0, p, 0) for p in range(FIRST, 4)] + [(0, p, 1) for p in range(4)]
+    added = {}
 
-    items.sort(key=lambda it: (it[0], it[1]))
-    load = {"V": 0.0, "S": 0.0}
-    for key, _i, E, fn, cost in items:
-        if E == "GATHER":
-            hs = []
-            for h in (0, 1):
-                e = "V" if load["V"] <= load["S"] else "S"
-                load[e] += 512 * KAPPA + 50
-                hs.append(e)
-            if fn == LAST and hs[0] != hs[1]:
-                for z in (0, 2):
-                    gather(fn, hs[0], z, z + 2)
-                    gather(fn, hs[1], 4 + z, 6 + z)
-            elif hs[0] == hs[1]:
-                gather(fn, hs[0], 0, 8)
+    def pieces(u):
+        i = units.index(u)
+        step = 2 if i == len(units) - 1 else 4 if i < 2 or i >= len(units) - PLAN["fine"] else 8
+        return [(u, z, z + step) for z in range(0, 8, step)]
+
+    def over(u, z0, z1):
+        return [q for q in pieces(u) if q[1] < z1 and q[2] > z0]
+
+    def col(u, z):
+        return 1024 * units.index(u) + 128 * z
+
+    def pick(q):
+        (d, p, w), z0, z1 = q
+
+        def fn(E):
+            need(E, ("xr", nx) if w else ("xl", 128), tok["off", listof[d, p]])
+            o = 128 * p + 64 * w
+            ind = (T.ws if w else T.wo)[:, 0:CH].indirect(T["off%d" % d][:, o + 8 * z0:o + 8 * z1])
+            out = T.gall[:, col(q[0], z0):col(q[0], z1)]
+            added[q] = E == "V" and w == 1
+            if added[q]:
+                need(E, *toks(over((d, p, 0), z0, z1)))
+                return em(E, V.tensor_tensor(out, ind, T.gall[:, col((d, p, 0), z0):col((d, p, 0), z1)], add))
+            return em(E, V.tensor_copy(out, ind) if E == "V" else S.activation(out, ind, Act.Copy))
+        task(q, "VS", 128 * (z1 - z0) * PLAN["kappa"] + 70, [("off", listof[d, p])], fn,
+             rel=PLAN["other"] if w else PLAN["own"], prio=units.index(q[0]) + z0 / 8.0)
+
+    for u in units:
+        for q in pieces(u):
+            pick(q)
+
+    def tiles(d, p, z):
+        second = over((d, p, 1), z, z + 1)[0]
+        return [T.gall[:, col((d, p, w), z):col((d, p, w), z) + 128] for w in ((1,) if added[second] else (0, 1))]
+
+    def both(d, p, z0, z1):
+        return over((d, p, 0), z0, z1) + over((d, p, 1), z0, z1)
+
+    nsent, nout = [0], [0]
+
+    def block(i, d, j, ps):
+        B = T["s%d" % (i % 2)]
+        c0, c1 = span(ps)
+        before = [("ev", i - 2)] if i >= 2 else []
+
+        def sums(p, h):
+            def fn(E):
+                need("P", *toks(["sel"] + before + both(d, p, 4 * h, 4 * h + 4)))
+                for r in (0, 1):
+                    c = 128 * p - c0 + 64 * h + 32 * r
+                    sels = (T.sel2, T.sel1) if d == 3 else (T.sel1, T.sel2)
+                    todo = [(t, sels[x]) for x in (0, 1) for t in tiles(d, p, 4 * h + r + 2 * x)]
+                    for x, (t, sel) in enumerate(todo):
+                        ins = P.matmul(B[:, c:c + 32], t, sel[:, :], x == 0, x == len(todo) - 1)
+                return em("P", ins)
+            return fn
+
+        mine = [("sum", d, p, h) for p in ps for h in (0, 1)]
+        for _s, _d, p, h in mine:
+            task(("sum", d, p, h), "P", 300, ["sel"] + before + both(d, p, 4 * h, 4 * h + 4), sums(p, h), prio=-3)
+
+        def evac(E):
+            need("V", *toks(mine))
+            return em("V", V.tensor_copy(T["snd%d" % d][:, c0:c1], B[:, 0:c1 - c0]))
+
+        def send(E):
+            to = peer[ONTO[d]]
+            need("G", tok["ev", i])
+            srcs = [T["snd%d" % d][:, c0:c1]]
+            if d == 2:
+                g.wait_ge(T.sem["ar1%d" % j], len(topo.engines(peer[ONTO[1]], core)))
+                srcs.append(T.rcv1[:, c0:c1])
+            g.remote_dma_fused([RemoteDMATransfer(dst_ids=[dst(to)], dma_engine_mask=topo.mask(core, to),
+                                                  remote_sem=T.sem["ar%d%d" % (d, j)], srcs=srcs, dsts=[T["rcv%d" % d][:, c0:c1]],
+                                                  alu_op=len(srcs) - 1)], local_sem=T.sem.sent)
+            nsent[0] += len(topo.engines(core, to))
+
+        task(("ev", i), "V", c1 - c0 + 25, mine, evac, prio=-8)
+        task(("send", d, j), "G", PLAN["sums"], [("ev", i)], send)
+
+    for i, (d, j) in enumerate([(d, j) for d in (1, 2, 3) for j in range(len(BLOCKS))]):
+        block(i, d, j, BLOCKS[j])
+
+    left = {}
+
+    def acc(bank, c, n, lhs, rhs):
+        left[bank] -= 1
+        return P.matmul(T[bank][:, c:c + n], lhs, rhs, False, left[bank] == 0)
+
+    def opening(b, n):
+        lists = ("off", max(i for i in range(len(chunks)) if 2 * i % 6 == b - b % 2))
+
+        def fn(E):
+            need("P", tok[lists])
+            return em("P", P.matmul(T["L%d" % b][:, 0:n], T.kb[0:1, :], T.row[0:1, 0:n], True, False))
+        task(("open", b), "P", n, [lists], fn, prio=-1)
+
+    def arrived(d, j, ps):
+        c0, c1 = span(ps)
+        mine = [gi for gi, x in enumerate(GROUPS) if x[0] in ps]
+        first = 3 * (3 - d)
+        last = [("open", first + gi) for gi in mine]
+        R = T["rcv%d" % d]
+        for gi in mine:
+            opening(first + gi, 128 * len(GROUPS[gi]))
+
+        def fn(E):
+            need("V", ("ar%d%d" % (d, j), len(topo.engines(peer[ONTO[d]], core))), *toks(last))
+            vs([], T["h%d" % d][:, c0:c1], R[:, c0:c1], 1.0 / 256, BASE - 127.5 / 256, mul, add)
+            for gi in mine:
+                a, b = span(GROUPS[gi])
+                t = vs([], T["L%d" % (first + gi)][:, 0:b - a], R[:, a:b], 256 * BASE, None, add)
+            return t
+        task(("arr", d, j), "V", 1.5 * (c1 - c0) + 75, [("send", d, j)] + last, fn, prio=-8)
+
+    for d in (2, 3):
+        for j, ps in enumerate(BLOCKS):
+            arrived(d, j, ps)
+
+    def group(gi, ps):
+        c0, c1 = span(ps)
+        n = c1 - c0
+        LO, HI = "L%d" % (3 + gi), "L%d" % gi
+        out = ("s0", "s1", "L3")[gi]
+        j = [x for x, b in enumerate(BLOCKS) if ps[0] in b][0]
+        arr = {LO: ("arr", 2, j), HI: ("arr", 3, j)}
+        parts = {LO: [], HI: []}
+
+        def early(E):
+            need("P", *toks(["id", arr[LO]]))
+            return em("P", acc(LO, 0, n, T.idn[:, :], T.h2[:, c0:c1]))
+
+        def fields(E):
+            need("P", *toks(["id", arr[LO], arr[HI]]))
+            acc(LO, 0, n, T.idp[:, :], T.h3[:, c0:c1])
+            acc(HI, 0, n, T.idp[:, :], T.h2[:, c0:c1])
+            return em("P", acc(HI, 0, n, T.idn[:, :], T.h3[:, c0:c1]))
+
+        def sums(bank, p, z0, deps):
+            def fn(E):
+                need("P", *toks(deps))
+                for z in (z0, z0 + 1):
+                    ts = tiles(0, p, z)
+                    left[bank] += len(ts) - 1
+                    for t in ts:
+                        ins = acc(bank, 128 * p - c0 + 64 * (z // 4) + 32 * (z % 2), 32, t, T.sel1[:, :])
+                return em("P", ins)
+            return fn
+
+        left[LO] = left[HI] = 2 + 4 * len(ps)
+        task(("early", gi), "P", n, ["id", arr[LO]], early, prio=-1)
+        task(("fields", gi), "P", 3 * n, ["id", arr[LO], arr[HI], ("early", gi)], fields, prio=-4)
+        for p in ps:
+            for z0 in (0, 2, 4, 6):
+                bank = HI if z0 % 4 else LO
+                deps = [arr[bank]] + both(0, p, z0, z0 + 2)
+                task(("own", p, z0), "P", 200, deps, sums(bank, p, z0, deps), prio=-3)
+                parts[bank].append(("own", p, z0))
+        side = {}
+
+        def clip(bank, C, top):
+            def fn(E):
+                side[bank] = E
+                ts = toks(parts[bank] + [("fields", gi)])
+                if E == "V":
+                    return vs(ts, C[:, c0:c1], T[bank][:, 0:n], top, top, Op.min, Op.subtract)
+                return sa(ts, C[:, c0:c1], T[bank][:, 0:n], Act.Relu, scale=-1.0, bias=top)
+            task(("clip", bank), "VS", n + 50, parts[bank] + [("fields", gi)], fn, prio=-7)
+
+        clip(LO, T.clo, BASE + 255.0)
+        clip(HI, T.chi, BASE + 255.0)
+        free = [("ev", 4 + gi)] if gi < 2 else [("clip", "L3")]
+
+        def turn(bank, C, zs):
+            def fn(E):
+                need("P", *toks([("clip", bank)] + free))
+                for p in ps:
+                    for z in zs:
+                        c = 128 * p + 64 * (z // 4) + 32 * (z % 2)
+                        ins = P.matmul(T[out][32 * p:32 * p + 32, 16 * z:16 * z + 16], C[:, c:c + 32],
+                                       T["sel" + side[bank]][:, :], True, True)
+                return em("P", ins)
+            task(("turn", bank), "P", n, [("clip", bank)] + free, fn, prio=-7)
+
+        turn(LO, T.clo, (0, 1, 4, 5))
+        turn(HI, T.chi, (2, 3, 6, 7))
+        r0, r1 = 32 * ps[0], 32 * ps[-1] + 32
+
+        def leave(E):
+            ts = toks([("turn", LO), ("turn", HI)])
+            if E == "V":
+                t = vs(ts, T.ysb[r0:r1, :], T[out][r0:r1, 0:128], 8 * 255.0, None, add)
             else:
-                gather(fn, hs[0], 0, 4)
-                gather(fn, hs[1], 4, 8)
-            continue
-        if E in load and key >= -0.3:
-            load[E] += cost
-        if fn is not None:
-            fn()
+                t = sa(ts, T.ysb[r0:r1, :], T[out][r0:r1, 0:128], bias=8 * 255.0)
+            need("Y", t)
+            g.sync.dma_start(T.y[r0:r1, :], T.ysb[r0:r1, :]).then_inc(T.sem.out, 16)
+            nout[0] += 16
+            return t
+        task(("leave", gi), "VS", 180, [("turn", LO), ("turn", HI)], leave, prio=-7)
+
+    for gi, ps in enumerate(GROUPS):
+        group(gi, ps)
+
+    fin = {}
+    free_at = {"V": 0.0, "S": 0.0, "P": 0.0, "G": 0.0}
+
+    def offer(E, name):
+        t = tasks[name]
+        deps, prio = list(t["deps"]), t["prio"]
+        if prio >= 0:
+            (d, p, w), z0, z1 = name
+            if prio > min(x["prio"] for y, x in tasks.items() if x["prio"] >= 0 and y not in fin) + PLAN["reach"]:
+                return None
+            if E == "V" and w:
+                deps += over((d, p, 0), z0, z1)
+            prio += PLAN["behind"] * (E == "V" and not w) + PLAN["ahead"] * (E == "S" and w)
+        if any(x not in fin for x in deps):
+            return None
+        return max([t["rel"], free_at[E]] + [fin[x] + PLAN["lag"] for x in deps]), prio
+
+    while len(fin) < len(tasks):
+        offers = [(o[0], o[1], E, i, name) for i, name in enumerate(tasks) if name not in fin
+                  for E in tasks[name]["on"] for o in [offer(E, name)] if o]
+        t0, _p, E, _i, name = min(offers, key=lambda o: o[:4])
+        tok[name] = tasks[name]["fn"](E)
+        fin[name] = t0 + tasks[name]["cost"]
+        free_at[E] = fin[name] if E != "G" else t0
     g.wait_ge(T.sem.out, nout[0])
     g.wait_ge(T.sem.ps, nps[0])
     g.wait_ge(T.sem.xs, nx)

@@ -8,11 +8,13 @@ CH = 4096
 OWNER = {1: 1, 2: 3, 3: 2}
 ONTO = {1: 2, 2: 3, 3: 2}
 FIRST = 3
-OWN_CHUNKS = ((0,), (1,), (2, 3))
-BLOCKS = ((0, 1), (2, 3))
+TWOS = ((0, 1), (2, 3))
+CHUNKS = (((0,), (1,), (2, 3)), ((0,), (1,), (2, 3)), TWOS, TWOS)
 GROUPS = ((0, 1), (2,), (3,))
-PLAN = dict(kappa=1.5, lag=150, own=3500, other=9500, lists=(5500, 9000, 16000), sums=4500, ahead=3.0, behind=2.0, fine=5,
-            reach=4.5)
+LATE = ((0, 1, 2, 3),)
+BLOCKS = {1: TWOS, 2: TWOS, 3: GROUPS}
+PLAN = dict(kappa=1.5, lag=150, own=1800, other=7000, lists1=4800, lists2=8000, lists3=11000, sums=3500, ahead=0.5, behind=2.0,
+            fine=6, early=5, finest=3, reach=3.5, hold=250)
 
 SCRATCH = {
     "wo": ("sbuf", [128, CH], "bfloat16"), "ws": ("sbuf", [128, CH], "bfloat16"),
@@ -25,6 +27,7 @@ SCRATCH = {
     "b3": ("sbuf", [128, 1], "float32"), "ec": ("sbuf", [128, 1], "float32"), "e2": ("sbuf", [128, 4], "float16"),
     "r": ("sbuf", [128, 512], "float16"), "l0": ("sbuf", [128, 128], "float16"), "lin": ("sbuf", [128, 512], "float16"),
     "row": ("sbuf", [128, 256], "bfloat16"), "ka": ("sbuf", [128, 128], "bfloat16"), "kb": ("sbuf", [128, 128], "bfloat16"),
+    "kz": ("sbuf", [128, 128], "bfloat16"),
     "x31": ("sbuf", [128, 32], "int32"), "x15": ("sbuf", [128, 16], "int32"),
     "sel1": ("sbuf", [128, 32], "bfloat16"), "sel2": ("sbuf", [128, 32], "bfloat16"),
     "selV": ("sbuf", [128, 16], "bfloat16"), "selS": ("sbuf", [128, 16], "bfloat16"),
@@ -43,7 +46,7 @@ for _d in range(4):
         SCRATCH["snd%d" % _d] = ("sbuf", [128, 512], "uint16")
         SCRATCH["rcv%d" % _d] = ("sbuf", [128, 512], "uint16")
 SEMAPHORES = ["V", "S", "P", "G", "par", "xl", "xs", "xr", "ps", "out", "sent"] + ["pr%d" % d for d in range(4)] \
-    + ["ar%d%d" % (d, b) for d in range(1, 4) for b in range(len(BLOCKS))]
+    + ["ar%d%d" % (d, b) for d in BLOCKS for b in range(len(BLOCKS[d]))]
 
 
 def rank_program(g, core, T, topo):
@@ -205,6 +208,7 @@ def rank_program(g, core, T, topo):
     def selections(E):
         vs([], T.x31[:, :], T.val[:, 0:32], 31, None, ands)
         x = vs([], T.x15[:, :], T.val[:, 0:16], 15, None, ands)
+        em("V", V.memset(T.kz[0:1, :], 0.0))
         vs([x], T.sel1[:, :], T.x31[:, :], 0, None, eq)
         vs([], T.sel2[:, :], T.x31[:, :], 0, 256.0, eq, mul)
         vs([], T.selV[:, :], T.x15[:, :], 0, None, eq)
@@ -220,7 +224,7 @@ def rank_program(g, core, T, topo):
     task("sel", "V", 600, [], selections, prio=-2)
     task("id", "V", 300, [], identities, rel=1500, prio=-2)
 
-    chunks = [(0, ps) for ps in OWN_CHUNKS] + [(d, ps) for d in (1, 2, 3) for ps in BLOCKS]
+    chunks = [(d, ps) for d in range(4) for ps in CHUNKS[d]]
     listof = {}
 
     def chunk(i, d, ps):
@@ -264,7 +268,7 @@ def rank_program(g, core, T, topo):
 
         order = [("a", i - 1)] if i else []
         task(("a", i), "P", 3 * n + 64 * first, before + order + [x for x in rs if x in tasks], eighths,
-             rel=PLAN["lists"][d - 1] if d else 0.0, prio=-5)
+             rel=PLAN["lists%d" % d] if d else 0.0, prio=-5)
         task(("z", i), "S", 2 * n + 200 + 110 * first, [("a", i)] + ([("z", i - 1)] if i else []), bend, prio=-5)
         task(("t", i), "P", 2 * n, [("z", i)], times, prio=-6)
         task(("off", i), "V", n + 25, [("t", i)], places, prio=-10)
@@ -282,8 +286,15 @@ def rank_program(g, core, T, topo):
 
     def pieces(u):
         i = units.index(u)
-        step = 2 if i == len(units) - 1 else 4 if i < 2 or i >= len(units) - PLAN["fine"] else 8
-        return [(u, z, z + step) for z in range(0, 8, step)]
+        cuts = (0, 4, 6, 8) if i >= len(units) - PLAN["finest"] else (0, 4, 8) if i < PLAN["early"] or i >= len(units) - PLAN["fine"] else (0, 8)
+        return [(u, a, b) for a, b in zip(cuts, cuts[1:])]
+
+    late = len(units) - 8 + FIRST
+    order = [q for u in units[:late] for q in pieces(u)]
+    order += [q for ps in LATE for up in (0, 1) for u in units[late:] if u[1] in ps for q in pieces(u) if (q[1] > 3) == up]
+    place = {}
+    for q in order:
+        place[q] = sum(x[2] - x[1] for x in place) / 8.0
 
     def over(u, z0, z1):
         return [q for q in pieces(u) if q[1] < z1 and q[2] > z0]
@@ -305,11 +316,10 @@ def rank_program(g, core, T, topo):
                 return em(E, V.tensor_tensor(out, ind, T.gall[:, col((d, p, 0), z0):col((d, p, 0), z1)], add))
             return em(E, V.tensor_copy(out, ind) if E == "V" else S.activation(out, ind, Act.Copy))
         task(q, "VS", 128 * (z1 - z0) * PLAN["kappa"] + 70, [("off", listof[d, p])], fn,
-             rel=PLAN["other"] if w else PLAN["own"], prio=units.index(q[0]) + z0 / 8.0)
+             rel=PLAN["other"] if w else PLAN["own"], prio=place[q])
 
-    for u in units:
-        for q in pieces(u):
-            pick(q)
+    for q in order:
+        pick(q)
 
     def tiles(d, p, z):
         second = over((d, p, 1), z, z + 1)[0]
@@ -325,21 +335,24 @@ def rank_program(g, core, T, topo):
         c0, c1 = span(ps)
         before = [("ev", i - 2)] if i >= 2 else []
 
-        def sums(p, h):
+        sels = (T.sel2, T.sel1) if d == 3 else (T.sel1, T.sel2)
+
+        def sums(p):
+            deps = ["sel"] + before + both(d, p, 0, 8)
+
             def fn(E):
-                need("P", *toks(["sel"] + before + both(d, p, 4 * h, 4 * h + 4)))
-                for r in (0, 1):
-                    c = 128 * p - c0 + 64 * h + 32 * r
-                    sels = (T.sel2, T.sel1) if d == 3 else (T.sel1, T.sel2)
-                    todo = [(t, sels[x]) for x in (0, 1) for t in tiles(d, p, 4 * h + r + 2 * x)]
+                need("P", *toks(deps))
+                for r in range(4):
+                    c = 128 * p - c0 + 32 * r
+                    todo = [(t, sels[x]) for x in (0, 1) for t in tiles(d, p, r + 4 * x)]
                     for x, (t, sel) in enumerate(todo):
                         ins = P.matmul(B[:, c:c + 32], t, sel[:, :], x == 0, x == len(todo) - 1)
                 return em("P", ins)
-            return fn
+            task(("sum", d, p), "P", lambda: 64 * sum(len(tiles(d, p, z)) for z in range(8)), deps, fn, prio=-3)
 
-        mine = [("sum", d, p, h) for p in ps for h in (0, 1)]
-        for _s, _d, p, h in mine:
-            task(("sum", d, p, h), "P", 300, ["sel"] + before + both(d, p, 4 * h, 4 * h + 4), sums(p, h), prio=-3)
+        mine = [("sum", d, p) for p in ps]
+        for p in ps:
+            sums(p)
 
         def evac(E):
             need("V", *toks(mine))
@@ -360,8 +373,9 @@ def rank_program(g, core, T, topo):
         task(("ev", i), "V", c1 - c0 + 25, mine, evac, prio=-8)
         task(("send", d, j), "G", PLAN["sums"], [("ev", i)], send)
 
-    for i, (d, j) in enumerate([(d, j) for d in (1, 2, 3) for j in range(len(BLOCKS))]):
-        block(i, d, j, BLOCKS[j])
+    blocks = [(d, j) for d in BLOCKS for j in range(len(BLOCKS[d]))]
+    for i, (d, j) in enumerate(blocks):
+        block(i, d, j, BLOCKS[d][j])
 
     left = {}
 
@@ -396,16 +410,15 @@ def rank_program(g, core, T, topo):
         task(("arr", d, j), "V", 1.5 * (c1 - c0) + 75, [("send", d, j)] + last, fn, prio=-8)
 
     for d in (2, 3):
-        for j, ps in enumerate(BLOCKS):
+        for j, ps in enumerate(BLOCKS[d]):
             arrived(d, j, ps)
 
     def group(gi, ps):
         c0, c1 = span(ps)
         n = c1 - c0
         LO, HI = "L%d" % (3 + gi), "L%d" % gi
-        out = ("s0", "s1", "L3")[gi]
-        j = [x for x, b in enumerate(BLOCKS) if ps[0] in b][0]
-        arr = {LO: ("arr", 2, j), HI: ("arr", 3, j)}
+        out = "s%d" % ((len(blocks) + gi) % 2) if gi < 2 else "L3"
+        arr = {b: ("arr", d, [x for x, y in enumerate(BLOCKS[d]) if ps[0] in y][0]) for b, d in ((LO, 2), (HI, 3))}
         parts = {LO: [], HI: []}
 
         def early(E):
@@ -425,7 +438,7 @@ def rank_program(g, core, T, topo):
                     ts = tiles(0, p, z)
                     left[bank] += len(ts) - 1
                     for t in ts:
-                        ins = acc(bank, 128 * p - c0 + 64 * (z // 4) + 32 * (z % 2), 32, t, T.sel1[:, :])
+                        ins = acc(bank, 128 * p - c0 + 32 * (z % 4), 32, t, T.sel1[:, :])
                 return em("P", ins)
             return fn
 
@@ -434,9 +447,10 @@ def rank_program(g, core, T, topo):
         task(("fields", gi), "P", 3 * n, ["id", arr[LO], arr[HI], ("early", gi)], fields, prio=-4)
         for p in ps:
             for z0 in (0, 2, 4, 6):
-                bank = HI if z0 % 4 else LO
+                bank = HI if z0 > 3 else LO
                 deps = [arr[bank]] + both(0, p, z0, z0 + 2)
-                task(("own", p, z0), "P", 200, deps, sums(bank, p, z0, deps), prio=-3)
+                task(("own", p, z0), "P", lambda p=p, z0=z0: 128 * len(tiles(0, p, z0)), deps, sums(bank, p, z0, deps),
+                     prio=-3 + 0.1 * gi)
                 parts[bank].append(("own", p, z0))
         side = {}
 
@@ -451,21 +465,21 @@ def rank_program(g, core, T, topo):
 
         clip(LO, T.clo, BASE + 255.0)
         clip(HI, T.chi, BASE + 255.0)
-        free = [("ev", 4 + gi)] if gi < 2 else [("clip", "L3")]
+        free = [("ev", len(blocks) - 2 + gi)] if gi < 2 else [("clip", "L3")]
 
         def turn(bank, C, zs):
             def fn(E):
                 need("P", *toks([("clip", bank)] + free))
                 for p in ps:
                     for z in zs:
-                        c = 128 * p + 64 * (z // 4) + 32 * (z % 2)
+                        c = 128 * p + 32 * (z % 4)
                         ins = P.matmul(T[out][32 * p:32 * p + 32, 16 * z:16 * z + 16], C[:, c:c + 32],
                                        T["sel" + side[bank]][:, :], True, True)
                 return em("P", ins)
             task(("turn", bank), "P", n, [("clip", bank)] + free, fn, prio=-7)
 
-        turn(LO, T.clo, (0, 1, 4, 5))
-        turn(HI, T.chi, (2, 3, 6, 7))
+        turn(LO, T.clo, range(4))
+        turn(HI, T.chi, range(4, 8))
         r0, r1 = 32 * ps[0], 32 * ps[-1] + 32
 
         def leave(E):
@@ -486,26 +500,29 @@ def rank_program(g, core, T, topo):
     fin = {}
     free_at = {"V": 0.0, "S": 0.0, "P": 0.0, "G": 0.0}
 
-    def offer(E, name):
+    def offer(E, name, oldest):
         t = tasks[name]
         deps, prio = list(t["deps"]), t["prio"]
         if prio >= 0:
             (d, p, w), z0, z1 = name
-            if prio > min(x["prio"] for y, x in tasks.items() if x["prio"] >= 0 and y not in fin) + PLAN["reach"]:
+            if prio > oldest + PLAN["reach"]:
                 return None
             if E == "V" and w:
                 deps += over((d, p, 0), z0, z1)
             prio += PLAN["behind"] * (E == "V" and not w) + PLAN["ahead"] * (E == "S" and w)
         if any(x not in fin for x in deps):
             return None
-        return max([t["rel"], free_at[E]] + [fin[x] + PLAN["lag"] for x in deps]), prio
+        t0 = max([t["rel"], free_at[E]] + [fin[x] + PLAN["lag"] for x in deps])
+        return t0 + PLAN["hold"] * (prio >= 0), prio, t0
 
     while len(fin) < len(tasks):
-        offers = [(o[0], o[1], E, i, name) for i, name in enumerate(tasks) if name not in fin
-                  for E in tasks[name]["on"] for o in [offer(E, name)] if o]
-        t0, _p, E, _i, name = min(offers, key=lambda o: o[:4])
+        oldest = min([place[q] for q in order if q not in fin] + [len(units)])
+        offers = [(o[0], o[1], E, i, name, o[2]) for i, name in enumerate(tasks) if name not in fin
+                  for E in tasks[name]["on"] for o in [offer(E, name, oldest)] if o]
+        _t, _p, E, _i, name, t0 = min(offers, key=lambda o: o[:4])
         tok[name] = tasks[name]["fn"](E)
-        fin[name] = t0 + tasks[name]["cost"]
+        cost = tasks[name]["cost"]
+        fin[name] = t0 + (cost if isinstance(cost, (int, float)) else cost())
         free_at[E] = fin[name] if E != "G" else t0
     g.wait_ge(T.sem.out, nout[0])
     g.wait_ge(T.sem.ps, nps[0])

from concourse.bass import DstId, RemoteDMATransfer
from concourse.mybir import AluOpType as Op, ActivationFunctionType as Act

MAGIC = 12582912.0
HALF = 2047.5 / 4096.0
BASE = 1536.0
CH = 4096
OWNER = {1: 1, 2: 3, 3: 2}
ONTO = {1: 2, 2: 3, 3: 2}
FIRST = 3
TWOS = ((0, 1), (2, 3))
CHUNKS = (((0,), (1,), (2, 3)), ((0,), (1,), (2, 3)), TWOS, TWOS)
GROUPS = ((0, 1), (2,), (3,))
LATE = ((0, 1, 2, 3),)
BLOCKS = {1: TWOS, 2: TWOS, 3: GROUPS}
PLAN = dict(kappa=1.5, lag=150, own=1800, other=7000, lists1=4800, lists2=8000, lists3=11000, sums=3500, ahead=0.5, behind=2.0,
            fine=6, early=5, finest=3, reach=3.5, hold=250)

SCRATCH = {
    "wo": ("sbuf", [128, CH], "bfloat16"), "ws": ("sbuf", [128, CH], "bfloat16"),
    "raw": ("sbuf", [128, 4], "int32"), "hq": ("sbuf", [128, 1], "int32"), "hf": ("sbuf", [128, 1], "float32"),
    "pf": ("sbuf", [128, 4], "float32"), "ones": ("sbuf", [128, 64], "float32"),
    "val": ("sbuf", [128, 64], "int32"), "xm": ("sbuf", [128, 14], "int32"), "e": ("sbuf", [128, 14], "float32"),
    "p0": ("sbuf", [128, 16], "float32"), "p1": ("sbuf", [128, 16], "float32"), "pat": ("sbuf", [128, 16], "float32"),
    "cm": ("sbuf", [128, 32], "float32"), "fc": ("sbuf", [128, 64], "float32"), "f": ("sbuf", [128, 128], "float32"),
    "m": ("sbuf", [128, 1], "float32"), "b1": ("sbuf", [128, 1], "float32"), "b2": ("sbuf", [128, 1], "float32"),
    "b3": ("sbuf", [128, 1], "float32"), "ec": ("sbuf", [128, 1], "float32"), "e2": ("sbuf", [128, 4], "float16"),
    "r": ("sbuf", [128, 512], "float16"), "l0": ("sbuf", [128, 128], "float16"), "lin": ("sbuf", [128, 512], "float16"),
    "row": ("sbuf", [128, 256], "bfloat16"), "ka": ("sbuf", [128, 128], "bfloat16"), "kb": ("sbuf", [128, 128], "bfloat16"),
    "kz": ("sbuf", [128, 128], "bfloat16"),
    "x31": ("sbuf", [128, 32], "int32"), "x15": ("sbuf", [128, 16], "int32"),
    "sel1": ("sbuf", [128, 32], "bfloat16"), "sel2": ("sbuf", [128, 32], "bfloat16"),
    "selV": ("sbuf", [128, 16], "bfloat16"), "selS": ("sbuf", [128, 16], "bfloat16"),
    "jd": ("sbuf", [128, 128], "int32"), "idp": ("sbuf", [128, 128], "float16"), "idn": ("sbuf", [128, 128], "float16"),
    "gall": ("sbuf", [128, 32768], "bfloat16"),
    "h2": ("sbuf", [128, 512], "float16"), "h3": ("sbuf", [128, 512], "float16"), "clo": ("sbuf", [128, 512], "bfloat16"), "chi": ("sbuf", [128, 512], "bfloat16"),
    "ysb": ("sbuf", [128, 128], "float32"),
}
for _n in ("L0", "L1", "L2", "L3", "L4", "L5", "s0", "s1"):
    SCRATCH[_n] = ("psum", [128, 512], "float32")
for _d in range(4):
    SCRATCH["w%d" % _d] = ("sbuf", [128, 512], "float32")
    SCRATCH["off%d" % _d] = ("sbuf", [128, 512], "uint16")
    SCRATCH["as%d" % _d] = ("sbuf", [128, 4], "float32")
    if _d:
        SCRATCH["snd%d" % _d] = ("sbuf", [128, 512], "uint16")
        SCRATCH["rcv%d" % _d] = ("sbuf", [128, 512], "uint16")
SEMAPHORES = ["V", "S", "P", "G", "par", "xl", "xs", "xr", "ps", "out", "sent"] + ["pr%d" % d for d in range(4)] \
    + ["ar%d%d" % (d, b) for d in BLOCKS for b in range(len(BLOCKS[d]))]


def rank_program(g, core, T, topo):
    me = T.rank_of(core)
    if me is None:
        return
    cores = list(T.cores)
    chips = []
    for c in cores:
        if topo.chip(c) not in chips:
            chips.append(topo.chip(c))
    ca = chips[0]
    cb = [c for c in chips[1:] if not topo.same_plane(ca, c)][0]
    chips = [ca, cb] + [[c for c in chips if topo.same_plane(x, c)][0] for x in (ca, cb)]
    on = [[c for c in cores if topo.chip(c) == ch] for ch in chips]
    k = chips.index(topo.chip(core))
    pos = on[k].index(core)
    sib = [c for c in on[k] if c != core][0]
    qs = (me, T.rank_of(sib))
    peer = [on[k ^ x][pos] for x in range(4)]

    V, S, P = g.vector, g.scalar, g.tensor
    queue = {"V": V, "S": S, "P": P, "G": g, "Y": g.sync}
    cnt = {"V": 0, "S": 0, "P": 0, "G": 0}
    seen = {}

    def em(E, ins):
        ins.then_inc(T.sem[E], 1)
        cnt[E] += 1
        return (E, cnt[E])

    def need(E, *toks):
        best = {}
        for tk in toks:
            if tk is not None:
                best[tk[0]] = max(best.get(tk[0], 0), tk[1])
        for s in best:
            if seen.get((E, s), 0) < best[s]:
                queue[E].wait_ge(T.sem[s], best[s])
                seen[(E, s)] = best[s]

    def vs(needs, out, in0, s1, s2, op0, op1=None):
        need("V", *needs)
        if op1 is None:
            return em("V", V.tensor_scalar(out, in0, s1, None, op0))
        return em("V", V.tensor_scalar(out, in0, s1, s2, op0, op1))

    def sa(needs, out, in_, func=Act.Identity, **kw):
        need("S", *needs)
        return em("S", S.activation(out, in_, func, **kw))

    def dst(c):
        rid, pid, _se = topo.addr(c)
        return DstId(rid=rid, pnc=pid)

    lo, hi = slice(0, 64), slice(64, 128)
    ands, eq, mul, add = Op.bitwise_and, Op.is_equal, Op.mult, Op.add

    one = em("V", V.memset(T.raw[96:128, :], 1))
    g.sync.dma_start(T.raw[lo, 0:4], T.de[:, :]).then_inc(T.sem.par, 16)
    for s in range(6):
        E = "YS"[s % 2]
        if s > 3:
            need(E, one)
        c = 0 if s in (3, 5) else 1
        queue[E].dma_start(T.raw[64 + 8 * s:72 + 8 * s, c:c + 2], T.pa[:, :]).then_inc(T.sem.par, 16)
    for c in range(4):
        for hh, q in ((0, g.sync), (1, S)):
            q.dma_start(T.wo[32 * c + 16 * hh:32 * c + 16 * hh + 16, :], T.x[:, CH * c:CH * c + CH]).then_inc(T.sem.xl, 16)

    imp = {"allow_small_or_imprecise_dtypes": True}
    i1 = em("G", g.iota(T.val[:, :], [[-1, 64]], 0, 1))
    need("G", i1)
    i2 = em("G", g.iota(T.p0[64:96, :], [[0, 4], [1, 4]], -2, 0, **imp))
    em("G", g.iota(T.fc[96:128, :], [[0, 8], [1, 8]], 0, 0, **imp))
    need("G", i2)
    i2 = em("G", g.iota(T.p1[64:96, :], [[4, 4], [0, 4]], -9, 0, **imp))
    need("G", i2)
    i3 = em("G", g.iota(T.fc[64:96, :], [[16, 8], [128, 8]], 9, 0, **imp))
    o1 = em("V", V.memset(T.ones[:, :], 1.0))
    em("V", V.memset(T.pat[:, :], 1.0))
    em("V", V.memset(T.row[0:1, :], 1.0))
    for j, (kk, v) in enumerate(((T.ka, 8 * MAGIC), (T.kb, MAGIC))):
        for h in (0, 1):
            kc = sa([o1], kk[0:1, 64 * h:64 * h + 64], T.ones[0:1, :], scale=v)
    for rows, parts in ((lo, ((64, 16, 48), (16, 8, 8), (8, 1, 7))), (hi, ((8, 2, 6), (2, 1, 1), (64, 8, 56)))):
        for (c0, c1), (end, step, bits) in zip(((0, 4), (4, 6), (6, 14)), parts):
            x = vs([i1], T.xm[rows, c0:c1], T.val[rows, 0:end:step], bits, None, ands)
    e = vs([x], T.e[:, :], T.xm[:, :], 0, None, eq)

    def st(s, rows=hi):
        return T.e[rows, 6 + s:7 + s]

    q64 = slice(64, 96)
    sa([e, i2], T.p0[q64, :], T.p0[q64, :], scale=st(1, q64), bias=1.0)
    t2 = sa([], T.p1[q64, :], T.p1[q64, :], scale=st(2, q64))
    vs([e], T.m[hi, :], st(0), st(4), 1.0 / 256, add, mul)
    b1 = vs([], T.b1[hi, :], st(1), st(2), 1.0 / 256, add, mul)
    ec = vs([], T.ec[hi, :], st(3), 128.0, st(5), mul, add)
    b2 = sa([b1], T.b2[hi, :], st(6), scale=-127.5 / 256, bias=T.b1[hi, :])
    for w in (0, 1):
        sa([], T.f[lo, 64 * w:64 * w + 64], T.ones[lo, :], scale=st(qs[w], lo))
    b3 = sa([b2], T.b3[hi, :], st(7), scale=-3.5, bias=T.b2[hi, :])
    for w in (0, 1):
        f = sa([b3, i3], T.f[hi, 64 * w:64 * w + 64], T.fc[hi, :], scale=T.m[hi, :], bias=T.b3[hi, :])
    need("V", t2)
    pat = em("V", V.tensor_tensor(T.pat[q64, :], T.p0[q64, :], T.p1[q64, :], add))
    e2 = vs([ec], T.e2[hi, :], T.e[hi, 0:4], T.ec[hi, :], 1.0 / 4096, mul, mul)
    for hh in (0, 1):
        cm = vs([pat], T.cm[:, 16 * hh:16 * hh + 16], T.pat[:, :], T.e[:, 4 + hh:5 + hh], None, mul)

    rh = {}

    def right(p):
        rh[p] = vs([f], T.r[:, 128 * p:128 * p + 128], T.f[:, :], T.e[:, p:p + 1], None, mul)
        return rh[p]

    V.wait_ge(T.sem.par, 16 * 7)
    vs([], T.hq[q64, :], T.raw[q64, 1:2], 7, None, Op.arith_shift_right)
    p1 = vs([], T.hq[96:128, :], T.raw[96:128, 1:2], 127, None, ands)
    vs([], T.pf[lo, :], T.raw[lo, :], 2048.0, None, Op.subtract)
    need("V", p1)
    p2 = em("V", V.tensor_copy(T.hf[hi, :], T.hq[hi, :]))
    right(0)
    p3 = vs([p2], T.pf[hi, :], T.ones[hi, 0:4], T.hf[hi, :], None, mul)
    for c in range(4):
        l0 = vs([p3, cm], T.l0[:, 32 * c:32 * c + 32], T.cm[:, :], T.pf[:, c:c + 1], None, mul)
    need("G", l0)
    nps = [0]
    came = {}
    for ds in ((1,), (2, 3)):
        m = topo.mask(core, peer[OWNER[ds[0]]]) & topo.mask(core, peer[OWNER[ds[-1]]])
        ne = bin(m).count("1")
        nps[0] += ne
        came.update({d: ne for d in ds})
        g.remote_dma_fused([RemoteDMATransfer(dst_ids=[dst(peer[OWNER[d]]) for d in ds], dma_engine_mask=m,
                                              remote_sem=T.sem["pr%d" % k], srcs=[T.l0[:, :]],
                                              dsts=[T.lin[:, 128 * d:128 * d + 128] for d in ds])], local_sem=T.sem.ps)
    need("G", i3)
    jd = em("G", g.iota(T.jd[:, :], [[-1, 128]], 0, 1))

    g.wait_ge(T.sem.xl, 128)
    rid, pid, _se = topo.addr(sib)
    g.remote_dma(T.ws[:, :], T.wo[:, :], T.sem.xr, T.sem.xs, pid, rid, topo.mask(core, sib))
    nx = len(topo.engines(core, sib))

    tasks = {}
    tok = {}

    def task(name, on_, cost, deps, fn, rel=0.0, prio=-1.0):
        tasks[name] = dict(on=on_, cost=cost, deps=list(deps), fn=fn, rel=rel, prio=prio)

    def toks(names):
        return [tok[n] for n in names]

    def span(ps):
        return 128 * ps[0], 128 * ps[-1] + 128

    def selections(E):
        vs([], T.x31[:, :], T.val[:, 0:32], 31, None, ands)
        x = vs([], T.x15[:, :], T.val[:, 0:16], 15, None, ands)
        em("V", V.memset(T.kz[0:1, :], 0.0))
        vs([x], T.sel1[:, :], T.x31[:, :], 0, None, eq)
        vs([], T.sel2[:, :], T.x31[:, :], 0, 256.0, eq, mul)
        vs([], T.selV[:, :], T.x15[:, :], 0, None, eq)
        return vs([], T.selS[:, :], T.x15[:, :], 0, -1.0, eq, mul)

    def identities(E):
        vs([jd], T.idp[:, :], T.jd[:, :], 0, None, eq)
        return vs([], T.idn[:, :], T.jd[:, :], 0, -256.0, eq, mul)

    tok["r", 0] = rh[0]
    for p in (1, 2, 3):
        task(("r", p), "V", 150, [], lambda E, p=p: right(p), prio=-9 + p)
    task("sel", "V", 600, [], selections, prio=-2)
    task("id", "V", 300, [], identities, rel=1500, prio=-2)

    chunks = [(d, ps) for d in range(4) for ps in CHUNKS[d]]
    listof = {}

    def chunk(i, d, ps):
        first = ps[0] == 0
        c0, c1 = span(ps)
        n = c1 - c0
        A, B = T["L%d" % (2 * i % 6)], T["L%d" % (2 * i % 6 + 1)]
        W, OFF, AS = [T["%s%d" % (nm, d)] for nm in ("w", "off", "as")]
        L = T.lin if d else T.l0
        before = [("off", i - 3)] if i >= 3 else []
        rs = [("r", p) for p in ps]

        def eighths(E):
            if d:
                need("P", ("pr%d" % (k ^ OWNER[d]), came[d]))
            need("P", l0, e2, kc, *toks(rs + before))
            if first:
                P.matmul(A[:, 256:260], L[hi, 128 * d:128 * d + 128], T.e2[hi, :], True, True)
            P.matmul(A[:, 0:n], L[:, 128 * d:128 * d + 128], T.r[:, c0:c1], True, False)
            tok["j", i] = em("P", P.matmul(A[:, 0:n], T.ka[0:1, :], T.row[0:1, 0:n], False, True))
            return em("P", P.matmul(B[:, 0:n], T.kb[0:1, :], T.row[0:1, 0:n], True, False))

        def bend(E):
            t = sa([tok["j", i]], W[:, c0:c1], A[:, 0:n], Act.Square, scale=0.125, bias=256.0 - MAGIC)
            if first:
                t = tok["as", d] = sa([], AS[:, :], A[:, 256:260], Act.Copy)
            need("S", tok["a", i])
            need("S", t)
            for p in ps:
                c = 128 * p
                t = sa([tok["as", d]], B[:, c - c0:c - c0 + 128], W[:, c:c + 128], bias=-HALF, scale=AS[:, p:p + 1])
            return t

        def times(E):
            need("P", tok["z", i])
            P.matmul(B[:, 0:n], T.kb[0:1, :], T.row[0:1, 0:n], False, False)
            return em("P", P.matmul(B[:, 0:n], L[0:120, 128 * d:128 * d + 128], T.r[0:120, c0:c1], False, True))

        def places(E):
            return vs([tok["t", i]], OFF[:, c0:c1], B[:, 0:n], MAGIC - 2048, None, Op.subtract)

        order = [("a", i - 1)] if i else []
        task(("a", i), "P", 3 * n + 64 * first, before + order + [x for x in rs if x in tasks], eighths,
             rel=PLAN["lists%d" % d] if d else 0.0, prio=-5)
        task(("z", i), "S", 2 * n + 200 + 110 * first, [("a", i)] + ([("z", i - 1)] if i else []), bend, prio=-5)
        task(("t", i), "P", 2 * n, [("z", i)], times, prio=-6)
        task(("off", i), "V", n + 25, [("t", i)], places, prio=-10)
        for p in ps:
            listof[d, p] = i

    for i, (d, ps) in enumerate(chunks):
        chunk(i, d, ps)

    units = [(0, p, 0) for p in range(FIRST)] + [(1, p, 0) for p in range(4)] + [(1, p, 1) for p in range(4)]
    for d in (2, 3):
        units += [(d, p, w) for p in range(4) for w in (0, 1)]
    units += [(0, p, 0) for p in range(FIRST, 4)] + [(0, p, 1) for p in range(4)]
    added = {}

    def pieces(u):
        i = units.index(u)
        cuts = (0, 4, 6, 8) if i >= len(units) - PLAN["finest"] else (0, 4, 8) if i < PLAN["early"] or i >= len(units) - PLAN["fine"] else (0, 8)
        return [(u, a, b) for a, b in zip(cuts, cuts[1:])]

    late = len(units) - 8 + FIRST
    order = [q for u in units[:late] for q in pieces(u)]
    order += [q for ps in LATE for up in (0, 1) for u in units[late:] if u[1] in ps for q in pieces(u) if (q[1] > 3) == up]
    place = {}
    for q in order:
        place[q] = sum(x[2] - x[1] for x in place) / 8.0

    def over(u, z0, z1):
        return [q for q in pieces(u) if q[1] < z1 and q[2] > z0]

    def col(u, z):
        return 1024 * units.index(u) + 128 * z

    def pick(q):
        (d, p, w), z0, z1 = q

        def fn(E):
            need(E, ("xr", nx) if w else ("xl", 128), tok["off", listof[d, p]])
            o = 128 * p + 64 * w
            ind = (T.ws if w else T.wo)[:, 0:CH].indirect(T["off%d" % d][:, o + 8 * z0:o + 8 * z1])
            out = T.gall[:, col(q[0], z0):col(q[0], z1)]
            added[q] = E == "V" and w == 1
            if added[q]:
                need(E, *toks(over((d, p, 0), z0, z1)))
                return em(E, V.tensor_tensor(out, ind, T.gall[:, col((d, p, 0), z0):col((d, p, 0), z1)], add))
            return em(E, V.tensor_copy(out, ind) if E == "V" else S.activation(out, ind, Act.Copy))
        task(q, "VS", 128 * (z1 - z0) * PLAN["kappa"] + 70, [("off", listof[d, p])], fn,
             rel=PLAN["other"] if w else PLAN["own"], prio=place[q])

    for q in order:
        pick(q)

    def tiles(d, p, z):
        second = over((d, p, 1), z, z + 1)[0]
        return [T.gall[:, col((d, p, w), z):col((d, p, w), z) + 128] for w in ((1,) if added[second] else (0, 1))]

    def both(d, p, z0, z1):
        return over((d, p, 0), z0, z1) + over((d, p, 1), z0, z1)

    nsent, nout = [0], [0]

    def block(i, d, j, ps):
        B = T["s%d" % (i % 2)]
        c0, c1 = span(ps)
        before = [("ev", i - 2)] if i >= 2 else []

        sels = (T.sel2, T.sel1) if d == 3 else (T.sel1, T.sel2)

        def sums(p):
            deps = ["sel"] + before + both(d, p, 0, 8)

            def fn(E):
                need("P", *toks(deps))
                for r in range(4):
                    c = 128 * p - c0 + 32 * r
                    todo = [(t, sels[x]) for x in (0, 1) for t in tiles(d, p, r + 4 * x)]
                    for x, (t, sel) in enumerate(todo):
                        ins = P.matmul(B[:, c:c + 32], t, sel[:, :], x == 0, x == len(todo) - 1)
                return em("P", ins)
            task(("sum", d, p), "P", lambda: 64 * sum(len(tiles(d, p, z)) for z in range(8)), deps, fn, prio=-3)

        mine = [("sum", d, p) for p in ps]
        for p in ps:
            sums(p)

        def evac(E):
            need("V", *toks(mine))
            return em("V", V.tensor_copy(T["snd%d" % d][:, c0:c1], B[:, 0:c1 - c0]))

        def send(E):
            to = peer[ONTO[d]]
            need("G", tok["ev", i])
            srcs = [T["snd%d" % d][:, c0:c1]]
            if d == 2:
                g.wait_ge(T.sem["ar1%d" % j], len(topo.engines(peer[ONTO[1]], core)))
                srcs.append(T.rcv1[:, c0:c1])
            g.remote_dma_fused([RemoteDMATransfer(dst_ids=[dst(to)], dma_engine_mask=topo.mask(core, to),
                                                  remote_sem=T.sem["ar%d%d" % (d, j)], srcs=srcs, dsts=[T["rcv%d" % d][:, c0:c1]],
                                                  alu_op=len(srcs) - 1)], local_sem=T.sem.sent)
            nsent[0] += len(topo.engines(core, to))

        task(("ev", i), "V", c1 - c0 + 25, mine, evac, prio=-8)
        task(("send", d, j), "G", PLAN["sums"], [("ev", i)], send)

    blocks = [(d, j) for d in BLOCKS for j in range(len(BLOCKS[d]))]
    for i, (d, j) in enumerate(blocks):
        block(i, d, j, BLOCKS[d][j])

    left = {}

    def acc(bank, c, n, lhs, rhs):
        left[bank] -= 1
        return P.matmul(T[bank][:, c:c + n], lhs, rhs, False, left[bank] == 0)

    def opening(b, n):
        lists = ("off", max(i for i in range(len(chunks)) if 2 * i % 6 == b - b % 2))

        def fn(E):
            need("P", tok[lists])
            return em("P", P.matmul(T["L%d" % b][:, 0:n], T.kb[0:1, :], T.row[0:1, 0:n], True, False))
        task(("open", b), "P", n, [lists], fn, prio=-1)

    def arrived(d, j, ps):
        c0, c1 = span(ps)
        mine = [gi for gi, x in enumerate(GROUPS) if x[0] in ps]
        first = 3 * (3 - d)
        last = [("open", first + gi) for gi in mine]
        R = T["rcv%d" % d]
        for gi in mine:
            opening(first + gi, 128 * len(GROUPS[gi]))

        def fn(E):
            need("V", ("ar%d%d" % (d, j), len(topo.engines(peer[ONTO[d]], core))), *toks(last))
            vs([], T["h%d" % d][:, c0:c1], R[:, c0:c1], 1.0 / 256, BASE - 127.5 / 256, mul, add)
            for gi in mine:
                a, b = span(GROUPS[gi])
                t = vs([], T["L%d" % (first + gi)][:, 0:b - a], R[:, a:b], 256 * BASE, None, add)
            return t
        task(("arr", d, j), "V", 1.5 * (c1 - c0) + 75, [("send", d, j)] + last, fn, prio=-8)

    for d in (2, 3):
        for j, ps in enumerate(BLOCKS[d]):
            arrived(d, j, ps)

    def group(gi, ps):
        c0, c1 = span(ps)
        n = c1 - c0
        LO, HI = "L%d" % (3 + gi), "L%d" % gi
        out = "s%d" % ((len(blocks) + gi) % 2) if gi < 2 else "L3"
        arr = {b: ("arr", d, [x for x, y in enumerate(BLOCKS[d]) if ps[0] in y][0]) for b, d in ((LO, 2), (HI, 3))}
        parts = {LO: [], HI: []}

        def early(E):
            need("P", *toks(["id", arr[LO]]))
            return em("P", acc(LO, 0, n, T.idn[:, :], T.h2[:, c0:c1]))

        def fields(E):
            need("P", *toks(["id", arr[LO], arr[HI]]))
            acc(LO, 0, n, T.idp[:, :], T.h3[:, c0:c1])
            acc(HI, 0, n, T.idp[:, :], T.h2[:, c0:c1])
            return em("P", acc(HI, 0, n, T.idn[:, :], T.h3[:, c0:c1]))

        def sums(bank, p, z0, deps):
            def fn(E):
                need("P", *toks(deps))
                for z in (z0, z0 + 1):
                    ts = tiles(0, p, z)
                    left[bank] += len(ts) - 1
                    for t in ts:
                        ins = acc(bank, 128 * p - c0 + 32 * (z % 4), 32, t, T.sel1[:, :])
                return em("P", ins)
            return fn

        left[LO] = left[HI] = 2 + 4 * len(ps)
        task(("early", gi), "P", n, ["id", arr[LO]], early, prio=-1)
        task(("fields", gi), "P", 3 * n, ["id", arr[LO], arr[HI], ("early", gi)], fields, prio=-4)
        for p in ps:
            for z0 in (0, 2, 4, 6):
                bank = HI if z0 > 3 else LO
                deps = [arr[bank]] + both(0, p, z0, z0 + 2)
                task(("own", p, z0), "P", lambda p=p, z0=z0: 128 * len(tiles(0, p, z0)), deps, sums(bank, p, z0, deps),
                     prio=-3 + 0.1 * gi)
                parts[bank].append(("own", p, z0))
        side = {}

        def clip(bank, C, top):
            def fn(E):
                side[bank] = E
                ts = toks(parts[bank] + [("fields", gi)])
                if E == "V":
                    return vs(ts, C[:, c0:c1], T[bank][:, 0:n], top, top, Op.min, Op.subtract)
                return sa(ts, C[:, c0:c1], T[bank][:, 0:n], Act.Relu, scale=-1.0, bias=top)
            task(("clip", bank), "VS", n + 50, parts[bank] + [("fields", gi)], fn, prio=-7)

        clip(LO, T.clo, BASE + 255.0)
        clip(HI, T.chi, BASE + 255.0)
        free = [("ev", len(blocks) - 2 + gi)] if gi < 2 else [("clip", "L3")]

        def turn(bank, C, zs):
            def fn(E):
                need("P", *toks([("clip", bank)] + free))
                for p in ps:
                    for z in zs:
                        c = 128 * p + 32 * (z % 4)
                        ins = P.matmul(T[out][32 * p:32 * p + 32, 16 * z:16 * z + 16], C[:, c:c + 32],
                                       T["sel" + side[bank]][:, :], True, True)
                return em("P", ins)
            task(("turn", bank), "P", n, [("clip", bank)] + free, fn, prio=-7)

        turn(LO, T.clo, range(4))
        turn(HI, T.chi, range(4, 8))
        r0, r1 = 32 * ps[0], 32 * ps[-1] + 32

        def leave(E):
            ts = toks([("turn", LO), ("turn", HI)])
            if E == "V":
                t = vs(ts, T.ysb[r0:r1, :], T[out][r0:r1, 0:128], 8 * 255.0, None, add)
            else:
                t = sa(ts, T.ysb[r0:r1, :], T[out][r0:r1, 0:128], bias=8 * 255.0)
            need("Y", t)
            g.sync.dma_start(T.y[r0:r1, :], T.ysb[r0:r1, :]).then_inc(T.sem.out, 16)
            nout[0] += 16
            return t
        task(("leave", gi), "VS", 180, [("turn", LO), ("turn", HI)], leave, prio=-7)

    for gi, ps in enumerate(GROUPS):
        group(gi, ps)

    fin = {}
    free_at = {"V": 0.0, "S": 0.0, "P": 0.0, "G": 0.0}

    def offer(E, name, oldest):
        t = tasks[name]
        deps, prio = list(t["deps"]), t["prio"]
        if prio >= 0:
            (d, p, w), z0, z1 = name
            if prio > oldest + PLAN["reach"]:
                return None
            if E == "V" and w:
                deps += over((d, p, 0), z0, z1)
            prio += PLAN["behind"] * (E == "V" and not w) + PLAN["ahead"] * (E == "S" and w)
        if any(x not in fin for x in deps):
            return None
        t0 = max([t["rel"], free_at[E]] + [fin[x] + PLAN["lag"] for x in deps])
        return t0 + PLAN["hold"] * (prio >= 0), prio, t0

    while len(fin) < len(tasks):
        oldest = min([place[q] for q in order if q not in fin] + [len(units)])
        offers = [(o[0], o[1], E, i, name, o[2]) for i, name in enumerate(tasks) if name not in fin
                  for E in tasks[name]["on"] for o in [offer(E, name, oldest)] if o]
        _t, _p, E, _i, name, t0 = min(offers, key=lambda o: o[:4])
        tok[name] = tasks[name]["fn"](E)
        cost = tasks[name]["cost"]
        fin[name] = t0 + (cost if isinstance(cost, (int, float)) else cost())
        free_at[E] = fin[name] if E != "G" else t0
    g.wait_ge(T.sem.out, nout[0])
    g.wait_ge(T.sem.ps, nps[0])
    g.wait_ge(T.sem.xs, nx)
    g.wait_ge(T.sem.sent, nsent[0])
    for E in ("V", "S", "P", "G"):
        need("G", (E, cnt[E]))
